import numpy as np
import ml_dtypes


def mxq(x, axis, fmt="e4m3"):
    dtype, down = {"e4m3": (ml_dtypes.float8_e4m3fn, 7), "e5m2": (ml_dtypes.float8_e5m2, 14)}[fmt]
    v = np.moveaxis(np.asarray(x, np.float32).astype(ml_dtypes.bfloat16).astype(np.float64), axis, -1)
    blocks = v.reshape(v.shape[:-1] + (-1, 32))
    amax = np.abs(blocks).max(-1, keepdims=True)
    byte = np.maximum(np.where(amax > 0, np.frexp(amax)[1] - 1 + 127, 0) - down, 1)
    scale = np.exp2(byte - 127.0)
    codes = (blocks / scale).astype(np.float32).astype(dtype).astype(np.float64)
    return np.moveaxis((codes * scale).reshape(v.shape), -1, axis)


WIDE = False


def mx_kscale(k):
    if not WIDE:
        return np.ones(k)
    levels = np.array([10, -10, 5, -5, 0])
    if k % 512:
        return np.exp2(np.random.permutation(np.resize(levels, k // 32))).repeat(32)
    a = np.empty((k // 512, 16))
    for p in range(k // 512):
        a[p, :8] = np.random.permutation(np.resize(levels, 8))
        for g in range(8):
            far = levels[np.abs(levels - a[p, g]) >= 10]
            a[p, g + 8] = far[np.random.randint(len(far))]
    return np.exp2(a.ravel()).repeat(32)


def f64(x):
    return np.asarray(x).astype(np.float64)


def striped(idx):
    return np.tile(idx.reshape(-1, 16).T, (8, 1)).astype(np.uint16)


def unstriped(offs):
    return offs[:16].T.reshape(-1).astype(np.int64)


E2M1 = np.array([0.0, 0.5, 1.0, 1.5, 2.0, 3.0, 4.0, 6.0, -0.0, -0.5, -1.0, -1.5, -2.0, -3.0, -4.0, -6.0])


def pack_weight(w, fmt):
    k, n = w.shape
    w = f64(np.asarray(w, np.float32).astype(ml_dtypes.bfloat16)).reshape(k // 32, 32, n)
    amax = np.abs(w).max(1)
    if fmt == "e4m3":
        byte = np.frexp(amax)[1] - 1 + 127 - 7
    else:
        mant, ex = np.frexp(amax / 6.0)
        byte = np.where(mant > 0.5, ex, ex - 1) + 127
    byte = np.clip(np.where(amax > 0, byte, 1), 1, 254)
    scaled = (w * np.exp2(127.0 - byte)[:, None, :]).reshape(k, n).astype(np.float32)
    by_word = np.ascontiguousarray(scaled.reshape(k // 512, 128, 4, n).transpose(0, 1, 3, 2))
    if fmt == "e4m3":
        words = by_word.astype(ml_dtypes.float8_e4m3fn).view(np.uint8)
    else:
        c = by_word.astype(ml_dtypes.float4_e2m1fn).view(np.uint8) & 0xF
        words = (c[..., 0::2] | (c[..., 1::2] << 4)).reshape(k // 512, 128, 2 * n)
    return np.ascontiguousarray(words), np.ascontiguousarray(byte.astype(np.uint8).reshape(k // 512, 16, n))


def unpack_weight(words, scales, fmt):
    g, _, n = scales.shape
    words = np.ascontiguousarray(words).reshape(g, 128, n, -1)
    if fmt == "e4m3":
        vals = words.view(ml_dtypes.float8_e4m3fn).astype(np.float64)
    else:
        nib = np.empty((g, 128, n, 4), np.uint8)
        nib[..., 0::2] = words & 0xF
        nib[..., 1::2] = words >> 4
        vals = E2M1[nib]
    vals = vals * np.repeat(np.exp2(scales.astype(np.float64) - 127.0), 8, axis=1)[..., None]
    return vals.transpose(0, 1, 3, 2).reshape(g * 512, n)


K, T, E, C, N = 512, 1024, 4, 256, 512


def by_expert(wq, xq):
    return np.concatenate([wq[e].T @ xq[:, e * C:(e + 1) * C] for e in range(E)], axis=1)


def setup_inputs():
    n = np.random.standard_normal
    s = mx_kscale(K)[:, None]
    w = [pack_weight(m, "e2m1") for m in n((E, K, N)) / np.sqrt(K) / s[None]]
    return {
        "xT": (n((K, T)) * s).astype(np.float32),
        "w_words": np.stack([m[0] for m in w]),
        "w_scales": np.stack([m[1] for m in w]),
        "b": (0.3 * n((N, E))).astype(np.float32),
        "gate": np.tile(np.random.uniform(0.2, 1.0, E * C), (N, 1)).astype(np.float32),
        "offs": striped(np.random.permutation(T)[:E * C]),
        "dst": striped(np.random.permutation(T)[:E * C]),
    }


def reference(xT, w_words, w_scales, b, gate, offs, dst):
    idx = unstriped(offs)
    w = np.stack([unpack_weight(w_words[e], w_scales[e], "e2m1") for e in range(E)])
    xq = mxq(f64(xT)[:, idx], 0, "e4m3")
    y = by_expert(w, xq)
    y = y + np.repeat(f64(b), C, axis=1)
    out = np.zeros((N, T))
    out[:, unstriped(dst)] = f64(gate) * y
    return out

@@ -1,0 +1,164 @@
+from contextlib import ExitStack
+
+import concourse.mybir as mybir
+
+K, T, E, C, N = 512, 1024, 4, 256, 512
+P = 128
+PACK = 4
+N_TILES = N // P
+
+FLOPS = 2 * K * N * E * C
+BYTES = 4 * (K * T + N * E + E * C + N * T) + E * (K * N // 2 + K // 32 * N) + 2 * 2 * P * (T // 16)
+
+F32 = mybir.dt.float32
+BF16 = mybir.dt.bfloat16
+U32 = mybir.dt.uint32
+I32 = mybir.dt.int32
+U16 = mybir.dt.uint16
+U8 = mybir.dt.uint8
+FP8X4 = mybir.dt.float8_e4m3fn_x4
+FP4X4 = mybir.dt.float4_e2m1fn_x4
+COPY = mybir.ActivationFunctionType.Copy
+IDENTITY = mybir.ActivationFunctionType.Identity
+MULT = mybir.AluOpType.mult
+ADD = mybir.AluOpType.add
+
+CHUNKS = ((0, 256), (256, 512), (512, 1024))
+
+
+def tile_moe_two_lin_bias_kernel(tc, xT, w_words, w_scales, b, gate, offs, dst, out):
+    nc = tc.nc
+    with ExitStack() as ctx:
+        held = ctx.enter_context(tc.tile_pool(name="held", bufs=1))
+        psum = ctx.enter_context(tc.psum_pool(name="psum", bufs=8))
+
+        offs_t = held.tile([P, T // 16], U16, name="offs_t")
+        dst_t = held.tile([P, T // 16], U16, name="dst_t")
+        ws = held.tile([P, E, N], U8, name="ws", align_bytes=64)
+        scale_rows = w_scales.rearrange("e a q n -> (a q) e n").bitcast(I32)
+        bias = held.tile([P, N_TILES, E], F32, name="bias")
+        x_rows = xT.rearrange("(p j) w -> p j w", j=PACK)
+        planes = [held.tile([P, T], F32, name=f"plane{j}") for j in range(PACK)]
+        words = held.tile([P, E, 2 * N], U8, name="words", align_bytes=64)
+        word_rows = w_words.rearrange("e a p n -> p (e a) n").bitcast(I32)
+        gate_t = held.tile([P, E * C], F32, name="gate_t")
+
+        nc.vector.memset(ws[:].bitcast(I32), 0)
+        nc.sync.dma_start(offs_t[:], offs)
+        nc.sync.dma_start(dst_t[:], dst)
+        for j in range(PACK):
+            nc.sync.dma_start(out=planes[j][:], in_=x_rows[:, j, :])
+        nc.sync.dma_start(out=words[:, 0:1].bitcast(I32), in_=word_rows[:, 0:1])
+        for q in range(4):
+            nc.sync.dma_start(out=ws[32 * q : 32 * q + 4].bitcast(I32), in_=scale_rows[4 * q : 4 * q + 4])
+        nc.sync.dma_start(out=bias[:], in_=b.rearrange("(i p) e -> p i e", p=P))
+        nc.sync.dma_start(out=gate_t[:, 0:C], in_=gate[0:P, 0:C])
+        nc.sync.dma_start(out=words[:, 1:E].bitcast(I32), in_=word_rows[:, 1:E])
+        nc.sync.dma_start(out=gate_t[:, C : E * C], in_=gate[0:P, C : E * C])
+
+        halves = [held.tile([P, T], BF16, name=f"half{j}") for j in range(3)]
+
+        def columns(listed, start, stop):
+            return listed[:, start // 16 : stop // 16]
+
+        def gather_vector(grouped, start, stop, j):
+            nc.vector.tensor_copy(grouped[:, :, j], planes[j][:].indirect(columns(offs_t, start, stop)))
+
+        def gather_scalar(grouped, start, stop, j):
+            nc.scalar.activation(grouped[:, :, j], halves[j][:].indirect(columns(offs_t, start, stop)), COPY)
+
+        def quantize(codes, scales, grouped, lo, hi):
+            nc.vector.quantize_mx(
+                out=codes[:, lo:hi].bitcast(FP8X4),
+                scales=scales[:, lo:hi],
+                in_=grouped[:, lo:hi, :].rearrange("p w j -> p (w j)"),
+            )
+
+        def multiply(acc, quantized, lo, hi, e, i):
+            codes, scales = quantized
+            nc.tensor.matmul_mx(
+                out=acc,
+                lhsT=words[:, e, 2 * P * i : 2 * P * (i + 1)].bitcast(FP4X4),
+                lhsT_scale=ws[:, e, P * i : P * (i + 1)],
+                rhs=codes[:, lo:hi].bitcast(FP8X4),
+                rhs_scale=scales[:, lo:hi],
+                start=True,
+                stop=True,
+            )
+
+        def add_bias(y, acc, e, i):
+            nc.scalar.activation(y, acc, IDENTITY, bias=bias[:, i, e : e + 1])
+
+        def scatter(window, y, start, stop):
+            nc.vector.tensor_tensor(window[:].indirect(columns(dst_t, start, stop)), y, gate_t[:, start:stop], MULT)
+
+        grouped0 = held.tile([P, C, PACK], BF16, name="grouped0", tag="g0", align_bytes=64)
+        grouped1 = held.tile([P, C, PACK], BF16, name="grouped1", tag="w2", align_bytes=64)
+        codes = [held.tile([P, n], U32, name=f"codes{c}", align_bytes=64) for c, n in enumerate((256, 256, 512))]
+        scales = [held.tile([P, n], U8, name=f"scales{c}", align_bytes=64) for c, n in enumerate((256, 256, 512))]
+        q = list(zip(codes, scales))
+        w0 = held.tile([P, T], F32, name="w0")
+        w1 = held.tile([P, T], F32, name="w1")
+        ya = held.tile([P, 128], F32, name="ya", tag="w3", align_bytes=64)
+        yb = held.tile([P, 128], F32, name="yb")
+        y01 = held.tile([P, C], F32, name="y01")
+        y02 = held.tile([P, C], F32, name="y02")
+        y3 = held.tile([P, 2 * C], F32, name="y3")
+        y1 = [held.tile([P, C], F32, name=f"y1{i}") for i in range(3)]
+        y2 = [held.tile([P, 2 * C], F32, name=f"y2{i}") for i in range(4)]
+
+        def gather0(j):
+            for lo, hi in ((0, 128), (128, 256)) if j == 3 else ((0, 256),):
+                nc.vector.tensor_copy(grouped0[:, lo:hi, j], planes[j][:].indirect(columns(offs_t, lo, hi)))
+
+        for j in range(3):
+            gather0(j)
+            nc.gpsimd.tensor_scalar(halves[j][:], planes[j][:], 1.0, 0.0, op0=MULT, op1=ADD)
+        gather0(3)
+        quantize(codes[0], scales[0], grouped0, 0, 128)
+        quantize(codes[0], scales[0], grouped0, 128, 256)
+        halves.append(held.tile([P, T], BF16, name="half3", tag="g0", align_bytes=64))
+        nc.vector.tensor_copy(halves[3][:], planes[3][:])
+        acc = psum.tile([P, 512], F32, name="acc")
+        multiply(acc[:, 0:128], q[0], 0, 128, 0, 0)
+        add_bias(ya[:], acc[:, 0:128], 0, 0)
+        for i, y in ((1, y01[:]), (2, y02[:]), (3, y3[:, 0:C])):
+            acc = psum.tile([P, 512], F32, name="acc")
+            multiply(acc[:, 0:C], q[0], 0, C, 0, i)
+            add_bias(y, acc[:, 0:C], 0, i)
+            if i == 1:
+                acc = psum.tile([P, 512], F32, name="acc")
+                multiply(acc[:, 0:128], q[0], 128, C, 0, 0)
+                add_bias(yb[:], acc[:, 0:128], 0, 0)
+        for j in range(PACK):
+            gather_scalar(grouped1, 256, 512, j)
+        scatter(w0, ya[:], 0, 128)
+        scatter(w1, y01[:], 0, 256)
+        scatter(w0, yb[:], 128, 256)
+        quantize(codes[1], scales[1], grouped1, 0, C)
+        for i, y in enumerate((y1[0][:], y1[1][:], y1[2][:], y3[:, C : 2 * C])):
+            acc = psum.tile([P, 512], F32, name="acc")
+            multiply(acc[:, 0:C], q[1], 0, C, 1, i)
+            add_bias(y, acc[:, 0:C], 1, i)
+        w2 = held.tile([P, T], F32, name="w2", tag="w2", align_bytes=64)
+        scatter(w2, y02[:], 0, 256)
+        grouped2 = held.tile([P, 2 * C, PACK], BF16, name="grouped2", tag="w3", align_bytes=64)
+        for j in range(PACK):
+            gather_scalar(grouped2, 512, 1024, j)
+        scatter(w0, y1[0][:], 256, 512)
+        scatter(w1, y1[1][:], 256, 512)
+        scatter(w2, y1[2][:], 256, 512)
+        quantize(codes[2], scales[2], grouped2, 0, 2 * C)
+        for i in range(N_TILES):
+            acc = psum.tile([P, 512], F32, name="acc")
+            for e in (2, 3):
+                lo = (e - 2) * C
+                multiply(acc[:, lo : lo + C], q[2], lo, lo + C, e, i)
+            for e in (2, 3):
+                lo = (e - 2) * C
+                add_bias(y2[i][:, lo : lo + C], acc[:, lo : lo + C], e, i)
+        w3 = held.tile([P, T], F32, name="w3", tag="w3", align_bytes=64)
+        scatter(w3, y3[:], 0, 512)
+        for i, window in enumerate((w0, w1, w2, w3)):
+            scatter(window, y2[i][:], 512, 1024)
+            nc.sync.dma_start(out=out[P * i : P * (i + 1), :], in_=window[:])

@@ -23,142 +23,153 @@ IDENTITY = mybir.ActivationFunctionType.Identity
 MULT = mybir.AluOpType.mult
 ADD = mybir.AluOpType.add
 
-CHUNKS = ((0, 256), (256, 512), (512, 1024))
+CHUNKS = ((0, 128), (128, 512), (512, 768), (768, 1024))
 
 
 def tile_moe_two_lin_bias_kernel(tc, xT, w_words, w_scales, b, gate, offs, dst, out):
     nc = tc.nc
     with ExitStack() as ctx:
         held = ctx.enter_context(tc.tile_pool(name="held", bufs=1))
-        psum = ctx.enter_context(tc.psum_pool(name="psum", bufs=8))
+        psum = ctx.enter_context(tc.psum_pool(name="psum", bufs=1))
 
         offs_t = held.tile([P, T // 16], U16, name="offs_t")
         dst_t = held.tile([P, T // 16], U16, name="dst_t")
-        ws = held.tile([P, E, N], U8, name="ws", align_bytes=64)
-        scale_rows = w_scales.rearrange("e a q n -> (a q) e n").bitcast(I32)
-        bias = held.tile([P, N_TILES, E], F32, name="bias")
+        groups = ((0, 1), (1, E))
+        ws = [held.tile([P, z - a, N], U8, name=f"ws{a}", align_bytes=64) for a, z in groups]
+        scale_rows = w_scales.rearrange("e a (q r) n -> r (a q) e n", r=4).bitcast(I32)
+        bias_rows = b.rearrange("(i p) e -> p i e", p=P)
+        experts = [(lo // C, (hi - 1) // C + 1) for lo, hi in CHUNKS]
+        early = [
+            held.tile([P, 2, z - a], F32, name=f"early{c}", tag=f"picked{c + 1}", align_bytes=64) for c, (a, z) in enumerate(experts)
+        ]
+        late = held.tile([P, 2, E], F32, name="late_bias")
+
+        def load_early(c):
+            with nc.allow_non_contiguous_dma(reason="one bias value for each output channel and expert"):
+                nc.sync.dma_start(out=early[c][:], in_=bias_rows[:, 0:2, experts[c][0] : experts[c][1]])
+
         x_rows = xT.rearrange("(p j) w -> p j w", j=PACK)
         planes = [held.tile([P, T], F32, name=f"plane{j}") for j in range(PACK)]
         words = held.tile([P, E, 2 * N], U8, name="words", align_bytes=64)
         word_rows = w_words.rearrange("e a p n -> p (e a) n").bitcast(I32)
+        opening = held.tile([P, 2, 2 * P], U8, name="opening", tag="late", align_bytes=64)
         gate_t = held.tile([P, E * C], F32, name="gate_t")
+        first = CHUNKS[0][1]
 
-        nc.vector.memset(ws[:].bitcast(I32), 0)
+        def load_scales(group):
+            for r in range(4):
+                nc.sync.dma_start(out=ws[group][r:P:32].bitcast(I32), in_=scale_rows[r][:, groups[group][0] : groups[group][1]])
+
+        for group in range(2):
+            nc.vector.memset(ws[group][:].bitcast(I32), 0)
+        nc.sync.dma_start(out=planes[0][:], in_=x_rows[:, 0, :])
         nc.sync.dma_start(offs_t[:], offs)
         nc.sync.dma_start(dst_t[:], dst)
-        for j in range(PACK):
+        load_early(0)
+        for j in range(1, PACK):
             nc.sync.dma_start(out=planes[j][:], in_=x_rows[:, j, :])
+        nc.sync.dma_start(out=opening[:].bitcast(I32), in_=word_rows[:, 0, 0:P].rearrange("p (i w) -> p i w", i=2))
+        load_scales(0)
+        nc.sync.dma_start(out=gate_t[:, 0:first], in_=gate[0:P, 0:first])
         nc.sync.dma_start(out=words[:, 0:1].bitcast(I32), in_=word_rows[:, 0:1])
-        for q in range(4):
-            nc.sync.dma_start(out=ws[32 * q : 32 * q + 4].bitcast(I32), in_=scale_rows[4 * q : 4 * q + 4])
-        nc.sync.dma_start(out=bias[:], in_=b.rearrange("(i p) e -> p i e", p=P))
-        nc.sync.dma_start(out=gate_t[:, 0:C], in_=gate[0:P, 0:C])
+        nc.sync.dma_start(out=late[:], in_=bias_rows[:, 2:4, :])
         nc.sync.dma_start(out=words[:, 1:E].bitcast(I32), in_=word_rows[:, 1:E])
-        nc.sync.dma_start(out=gate_t[:, C : E * C], in_=gate[0:P, C : E * C])
+        load_scales(1)
+        load_early(1)
+        nc.sync.dma_start(out=gate_t[:, first : E * C], in_=gate[0:P, first : E * C])
+        load_early(2)
+        load_early(3)
 
-        halves = [held.tile([P, T], BF16, name=f"half{j}") for j in range(3)]
+        windows = {}
+        codes = {}
+        scales = [held.tile([P, hi - lo], U8, name=f"scales{lo}", align_bytes=64) for lo, hi in CHUNKS]
 
-        def columns(listed, start, stop):
-            return listed[:, start // 16 : stop // 16]
+        def columns(listed, c):
+            return listed[:, CHUNKS[c][0] // 16 : CHUNKS[c][1] // 16]
 
-        def gather_vector(grouped, start, stop, j):
-            nc.vector.tensor_copy(grouped[:, :, j], planes[j][:].indirect(columns(offs_t, start, stop)))
+        def expert_runs(c):
+            lo, hi = CHUNKS[c]
+            cuts = [lo] + [s for s in range(C, E * C, C) if lo < s < hi] + [hi]
+            return [(a // C, a - lo, z - lo) for a, z in zip(cuts, cuts[1:])]
 
-        def gather_scalar(grouped, start, stop, j):
-            nc.scalar.activation(grouped[:, :, j], halves[j][:].indirect(columns(offs_t, start, stop)), COPY)
+        def quantize(c, grouped):
+            codes[c] = held.tile([P, CHUNKS[c][1] - CHUNKS[c][0]], U32, name=f"codes{c}", tag=f"y{c - 1}_0", align_bytes=64)
+            for part, (e, lo, hi) in zip(grouped, expert_runs(c)):
+                nc.vector.quantize_mx(
+                    out=codes[c][:, lo:hi].bitcast(FP8X4),
+                    scales=scales[c][:, lo:hi],
+                    in_=part[:].rearrange("p w j -> p (w j)"),
+                )
 
-        def quantize(codes, scales, grouped, lo, hi):
-            nc.vector.quantize_mx(
-                out=codes[:, lo:hi].bitcast(FP8X4),
-                scales=scales[:, lo:hi],
-                in_=grouped[:, lo:hi, :].rearrange("p w j -> p (w j)"),
+        def product(c, i):
+            y_tag = f"picked{c + 1}" if i == 2 and 0 < c < len(CHUNKS) - 1 else f"y{c}_{i}"
+            acc = psum.tile([P, 512], F32, name="acc", tag=f"bank{i if c == 0 else min(i, 1)}")
+            y = held.tile([P, CHUNKS[c][1] - CHUNKS[c][0]], F32, name=f"y{c}_{i}", tag=y_tag, align_bytes=64)
+            for e, lo, hi in expert_runs(c):
+                nc.tensor.matmul_mx(
+                    out=acc[:, lo:hi],
+                    lhsT=(opening[:, i, :] if c == 0 and i < 2 else words[:, e, 2 * P * i : 2 * P * (i + 1)]).bitcast(FP4X4),
+                    lhsT_scale=ws[min(e, 1)][:, e - min(e, 1), P * i : P * (i + 1)],
+                    rhs=codes[c][:, lo:hi].bitcast(FP8X4),
+                    rhs_scale=scales[c][:, lo:hi],
+                    start=True,
+                    stop=True,
+                )
+            for e, lo, hi in expert_runs(c):
+                column = early[c][:, i, e - experts[c][0] : e - experts[c][0] + 1] if i < 2 else late[:, i - 2, e : e + 1]
+                nc.scalar.activation(y[:, lo:hi], acc[:, lo:hi], IDENTITY, bias=column)
+            return y
+
+        def scatter(c, i, y):
+            lo, hi = CHUNKS[c]
+            if c == 0:
+                windows[i] = held.tile([P, T], F32, name=f"window{i}", tag=f"window{i}", align_bytes=64)
+            nc.vector.tensor_tensor(windows[i][:].indirect(columns(dst_t, c)), y[:], gate_t[:, lo:hi], MULT)
+            if c == len(CHUNKS) - 1:
+                nc.sync.dma_start(out=out[P * i : P * (i + 1), :], in_=windows[i][:])
+
+        def gather(c, grouped, j):
+            for part, (e, lo, hi) in zip(grouped, expert_runs(c)):
+                picks = offs_t[:, (CHUNKS[c][0] + lo) // 16 : (CHUNKS[c][0] + hi) // 16]
+                nc.scalar.activation(part[:, :, j], halves[j][:].indirect(picks), COPY)
+
+        def grouped_tile(c):
+            return held.tile([P, CHUNKS[c][1] - CHUNKS[c][0], PACK], BF16, name=f"grouped{c}", align_bytes=64)
+
+        def gather_then_interleave(c):
+            n = CHUNKS[c][1] - CHUNKS[c][0]
+            picked = held.tile([P, PACK, n], BF16, name=f"picked{c}", tag=f"picked{c}", align_bytes=64)
+            for j in range(PACK):
+                nc.scalar.activation(picked[:, j, :], halves[j][:].indirect(columns(offs_t, c)), COPY)
+            woven = grouped_tile(c)
+            nc.scalar.copy(
+                woven[:].rearrange("p (s u) j -> p s j u", u=4), picked[:].rearrange("p j (s u) -> p s j u", u=4)
             )
+            return [woven]
 
-        def multiply(acc, quantized, lo, hi, e, i):
-            codes, scales = quantized
-            nc.tensor.matmul_mx(
-                out=acc,
-                lhsT=words[:, e, 2 * P * i : 2 * P * (i + 1)].bitcast(FP4X4),
-                lhsT_scale=ws[:, e, P * i : P * (i + 1)],
-                rhs=codes[:, lo:hi].bitcast(FP8X4),
-                rhs_scale=scales[:, lo:hi],
-                start=True,
-                stop=True,
-            )
-
-        def add_bias(y, acc, e, i):
-            nc.scalar.activation(y, acc, IDENTITY, bias=bias[:, i, e : e + 1])
-
-        def scatter(window, y, start, stop):
-            nc.vector.tensor_tensor(window[:].indirect(columns(dst_t, start, stop)), y, gate_t[:, start:stop], MULT)
-
-        grouped0 = held.tile([P, C, PACK], BF16, name="grouped0", tag="g0", align_bytes=64)
-        grouped1 = held.tile([P, C, PACK], BF16, name="grouped1", tag="w2", align_bytes=64)
-        codes = [held.tile([P, n], U32, name=f"codes{c}", align_bytes=64) for c, n in enumerate((256, 256, 512))]
-        scales = [held.tile([P, n], U8, name=f"scales{c}", align_bytes=64) for c, n in enumerate((256, 256, 512))]
-        q = list(zip(codes, scales))
-        w0 = held.tile([P, T], F32, name="w0")
-        w1 = held.tile([P, T], F32, name="w1")
-        ya = held.tile([P, 128], F32, name="ya", tag="w3", align_bytes=64)
-        yb = held.tile([P, 128], F32, name="yb")
-        y01 = held.tile([P, C], F32, name="y01")
-        y02 = held.tile([P, C], F32, name="y02")
-        y3 = held.tile([P, 2 * C], F32, name="y3")
-        y1 = [held.tile([P, C], F32, name=f"y1{i}") for i in range(3)]
-        y2 = [held.tile([P, 2 * C], F32, name=f"y2{i}") for i in range(4)]
-
-        def gather0(j):
-            for lo, hi in ((0, 128), (128, 256)) if j == 3 else ((0, 256),):
-                nc.vector.tensor_copy(grouped0[:, lo:hi, j], planes[j][:].indirect(columns(offs_t, lo, hi)))
-
-        for j in range(3):
-            gather0(j)
-            nc.gpsimd.tensor_scalar(halves[j][:], planes[j][:], 1.0, 0.0, op0=MULT, op1=ADD)
-        gather0(3)
-        quantize(codes[0], scales[0], grouped0, 0, 128)
-        quantize(codes[0], scales[0], grouped0, 128, 256)
-        halves.append(held.tile([P, T], BF16, name="half3", tag="g0", align_bytes=64))
+        grouped0 = held.tile([P, first, PACK], BF16, name="grouped0", align_bytes=64)
+        grouped = [
+            held.tile([P, hi - lo, PACK], BF16, name=f"second{e}", tag=f"window{2 + e}", align_bytes=64)
+            for e, lo, hi in expert_runs(1)
+        ]
+        halves = []
+        for j in range(PACK - 1):
+            halves.append(held.tile([P, T], BF16, name=f"half{j}"))
+            nc.vector.tensor_copy(halves[j][:], planes[j][:])
+            nc.vector.tensor_copy(grouped0[:, :, j], planes[j][:].indirect(columns(offs_t, 0)))
+            gather(1, grouped, j)
+        nc.vector.tensor_copy(grouped0[:, :, 3], planes[3][:].indirect(columns(offs_t, 0)))
+        quantize(0, [grouped0])
+        halves.append(held.tile([P, T], BF16, name="half3", tag="late", align_bytes=64))
         nc.vector.tensor_copy(halves[3][:], planes[3][:])
-        acc = psum.tile([P, 512], F32, name="acc")
-        multiply(acc[:, 0:128], q[0], 0, 128, 0, 0)
-        add_bias(ya[:], acc[:, 0:128], 0, 0)
-        for i, y in ((1, y01[:]), (2, y02[:]), (3, y3[:, 0:C])):
-            acc = psum.tile([P, 512], F32, name="acc")
-            multiply(acc[:, 0:C], q[0], 0, C, 0, i)
-            add_bias(y, acc[:, 0:C], 0, i)
-            if i == 1:
-                acc = psum.tile([P, 512], F32, name="acc")
-                multiply(acc[:, 0:128], q[0], 128, C, 0, 0)
-                add_bias(yb[:], acc[:, 0:128], 0, 0)
-        for j in range(PACK):
-            gather_scalar(grouped1, 256, 512, j)
-        scatter(w0, ya[:], 0, 128)
-        scatter(w1, y01[:], 0, 256)
-        scatter(w0, yb[:], 128, 256)
-        quantize(codes[1], scales[1], grouped1, 0, C)
-        for i, y in enumerate((y1[0][:], y1[1][:], y1[2][:], y3[:, C : 2 * C])):
-            acc = psum.tile([P, 512], F32, name="acc")
-            multiply(acc[:, 0:C], q[1], 0, C, 1, i)
-            add_bias(y, acc[:, 0:C], 1, i)
-        w2 = held.tile([P, T], F32, name="w2", tag="w2", align_bytes=64)
-        scatter(w2, y02[:], 0, 256)
-        grouped2 = held.tile([P, 2 * C, PACK], BF16, name="grouped2", tag="w3", align_bytes=64)
-        for j in range(PACK):
-            gather_scalar(grouped2, 512, 1024, j)
-        scatter(w0, y1[0][:], 256, 512)
-        scatter(w1, y1[1][:], 256, 512)
-        scatter(w2, y1[2][:], 256, 512)
-        quantize(codes[2], scales[2], grouped2, 0, 2 * C)
-        for i in range(N_TILES):
-            acc = psum.tile([P, 512], F32, name="acc")
-            for e in (2, 3):
-                lo = (e - 2) * C
-                multiply(acc[:, lo : lo + C], q[2], lo, lo + C, e, i)
-            for e in (2, 3):
-                lo = (e - 2) * C
-                add_bias(y2[i][:, lo : lo + C], acc[:, lo : lo + C], e, i)
-        w3 = held.tile([P, T], F32, name="w3", tag="w3", align_bytes=64)
-        scatter(w3, y3[:], 0, 512)
-        for i, window in enumerate((w0, w1, w2, w3)):
-            scatter(window, y2[i][:], 512, 1024)
-            nc.sync.dma_start(out=out[P * i : P * (i + 1), :], in_=window[:])
+        for c in range(len(CHUNKS)):
+            for i in (0, 1):
+                scatter(c, i, product(c, i))
+            if c + 1 < len(CHUNKS):
+                if c > 0:
+                    grouped = gather_then_interleave(c + 1)
+                else:
+                    gather(1, grouped, 3)
+                quantize(c + 1, grouped)
+            for i in (2, 3):
+                scatter(c, i, product(c, i))

@@ -22,8 +22,7 @@ COPY = mybir.ActivationFunctionType.Copy
 IDENTITY = mybir.ActivationFunctionType.Identity
 MULT = mybir.AluOpType.mult
 ADD = mybir.AluOpType.add
-
-CHUNKS = ((0, 128), (128, 512), (512, 768), (768, 1024))
+HALF = C // 2
 
 
 def tile_moe_two_lin_bias_kernel(tc, xT, w_words, w_scales, b, gate, offs, dst, out):
@@ -32,29 +31,27 @@ def tile_moe_two_lin_bias_kernel(tc, xT, w_words, w_scales, b, gate, offs, dst, 
         held = ctx.enter_context(tc.tile_pool(name="held", bufs=1))
         psum = ctx.enter_context(tc.psum_pool(name="psum", bufs=1))
 
+        def tile(shape, dtype, name, slot=None):
+            return held.tile(shape, dtype, name=name, tag=slot or name, align_bytes=64)
+
         offs_t = held.tile([P, T // 16], U16, name="offs_t")
         dst_t = held.tile([P, T // 16], U16, name="dst_t")
-        groups = ((0, 1), (1, E))
-        ws = [held.tile([P, z - a, N], U8, name=f"ws{a}", align_bytes=64) for a, z in groups]
-        scale_rows = w_scales.rearrange("e a (q r) n -> r (a q) e n", r=4).bitcast(I32)
-        bias_rows = b.rearrange("(i p) e -> p i e", p=P)
-        experts = [(lo // C, (hi - 1) // C + 1) for lo, hi in CHUNKS]
-        early = [
-            held.tile([P, 2, z - a], F32, name=f"early{c}", tag=f"picked{c + 1}", align_bytes=64) for c, (a, z) in enumerate(experts)
-        ]
-        late = held.tile([P, 2, E], F32, name="late_bias")
-
-        def load_early(c):
-            with nc.allow_non_contiguous_dma(reason="one bias value for each output channel and expert"):
-                nc.sync.dma_start(out=early[c][:], in_=bias_rows[:, 0:2, experts[c][0] : experts[c][1]])
-
         x_rows = xT.rearrange("(p j) w -> p j w", j=PACK)
-        planes = [held.tile([P, T], F32, name=f"plane{j}") for j in range(PACK)]
-        words = held.tile([P, E, 2 * N], U8, name="words", align_bytes=64)
+        planes = [tile([P, T], F32, f"plane{j}") for j in range(PACK)]
         word_rows = w_words.rearrange("e a p n -> p (e a) n").bitcast(I32)
-        opening = held.tile([P, 2, 2 * P], U8, name="opening", tag="late", align_bytes=64)
-        gate_t = held.tile([P, E * C], F32, name="gate_t")
-        first = CHUNKS[0][1]
+        words = tile([P, E, 2 * N], U8, "words")
+        scale_rows = w_scales.rearrange("e a (q r) n -> r (a q) e n", r=4).bitcast(I32)
+        groups = ((0, 1), (1, E))
+        ws = [tile([P, z - a, N], U8, f"ws{a}") for a, z in groups]
+        bias_rows = b.rearrange("(i p) e -> p i e", p=P)
+        opening_bias = tile([P, 2, 1], F32, "opening_bias", "picked1")
+        early = [tile([P, 2, 1], F32, f"early{e}", f"picked{e + 1}" if e else None) for e in range(E)]
+        late = tile([P, 2, E], F32, "late_bias")
+        gate_t = tile([P, E * C], F32, "gate_t")
+
+        def load_bias(columns, e):
+            with nc.allow_non_contiguous_dma(reason="one bias value for each output channel"):
+                nc.sync.dma_start(out=columns[:], in_=bias_rows[:, 0:2, e : e + 1])
 
         def load_scales(group):
             for r in range(4):
@@ -65,111 +62,90 @@ def tile_moe_two_lin_bias_kernel(tc, xT, w_words, w_scales, b, gate, offs, dst, 
         nc.sync.dma_start(out=planes[0][:], in_=x_rows[:, 0, :])
         nc.sync.dma_start(offs_t[:], offs)
         nc.sync.dma_start(dst_t[:], dst)
-        load_early(0)
+        load_bias(opening_bias, 0)
         for j in range(1, PACK):
             nc.sync.dma_start(out=planes[j][:], in_=x_rows[:, j, :])
-        nc.sync.dma_start(out=opening[:].bitcast(I32), in_=word_rows[:, 0, 0:P].rearrange("p (i w) -> p i w", i=2))
-        load_scales(0)
-        nc.sync.dma_start(out=gate_t[:, 0:first], in_=gate[0:P, 0:first])
         nc.sync.dma_start(out=words[:, 0:1].bitcast(I32), in_=word_rows[:, 0:1])
+        load_scales(0)
+        nc.sync.dma_start(out=gate_t[:, 0:C], in_=gate[0:P, 0:C])
+        load_bias(early[0], 0)
         nc.sync.dma_start(out=late[:], in_=bias_rows[:, 2:4, :])
         nc.sync.dma_start(out=words[:, 1:E].bitcast(I32), in_=word_rows[:, 1:E])
         load_scales(1)
-        load_early(1)
-        nc.sync.dma_start(out=gate_t[:, first : E * C], in_=gate[0:P, first : E * C])
-        load_early(2)
-        load_early(3)
+        load_bias(early[1], 1)
+        nc.sync.dma_start(out=gate_t[:, C : E * C], in_=gate[0:P, C : E * C])
+        for e in range(2, E):
+            load_bias(early[e], e)
 
-        windows = {}
+        halves = [tile([P, T], BF16, f"half{j}") for j in range(PACK)]
+        windows = [tile([P, T], F32, f"window{i}") for i in range(N_TILES)]
+        scales = [tile([P, C], U8, f"scales{e}") for e in range(E)]
         codes = {}
-        scales = [held.tile([P, hi - lo], U8, name=f"scales{lo}", align_bytes=64) for lo, hi in CHUNKS]
 
-        def columns(listed, c):
-            return listed[:, CHUNKS[c][0] // 16 : CHUNKS[c][1] // 16]
+        def entries(listed, lo, hi):
+            return listed[:, lo // 16 : hi // 16]
 
-        def expert_runs(c):
-            lo, hi = CHUNKS[c]
-            cuts = [lo] + [s for s in range(C, E * C, C) if lo < s < hi] + [hi]
-            return [(a // C, a - lo, z - lo) for a, z in zip(cuts, cuts[1:])]
+        def quantize(e, woven, lo, hi):
+            nc.vector.quantize_mx(
+                out=codes[e][:, lo:hi].bitcast(FP8X4),
+                scales=scales[e][:, lo:hi],
+                in_=woven[:, lo:hi, :].rearrange("p w j -> p (w j)"),
+            )
 
-        def quantize(c, grouped):
-            codes[c] = held.tile([P, CHUNKS[c][1] - CHUNKS[c][0]], U32, name=f"codes{c}", tag=f"y{c - 1}_0", align_bytes=64)
-            for part, (e, lo, hi) in zip(grouped, expert_runs(c)):
-                nc.vector.quantize_mx(
-                    out=codes[c][:, lo:hi].bitcast(FP8X4),
-                    scales=scales[c][:, lo:hi],
-                    in_=part[:].rearrange("p w j -> p (w j)"),
-                )
-
-        def product(c, i):
-            y_tag = f"picked{c + 1}" if i == 2 and 0 < c < len(CHUNKS) - 1 else f"y{c}_{i}"
-            acc = psum.tile([P, 512], F32, name="acc", tag=f"bank{i if c == 0 else min(i, 1)}")
-            y = held.tile([P, CHUNKS[c][1] - CHUNKS[c][0]], F32, name=f"y{c}_{i}", tag=y_tag, align_bytes=64)
-            for e, lo, hi in expert_runs(c):
-                nc.tensor.matmul_mx(
-                    out=acc[:, lo:hi],
-                    lhsT=(opening[:, i, :] if c == 0 and i < 2 else words[:, e, 2 * P * i : 2 * P * (i + 1)]).bitcast(FP4X4),
-                    lhsT_scale=ws[min(e, 1)][:, e - min(e, 1), P * i : P * (i + 1)],
-                    rhs=codes[c][:, lo:hi].bitcast(FP8X4),
-                    rhs_scale=scales[c][:, lo:hi],
-                    start=True,
-                    stop=True,
-                )
-            for e, lo, hi in expert_runs(c):
-                column = early[c][:, i, e - experts[c][0] : e - experts[c][0] + 1] if i < 2 else late[:, i - 2, e : e + 1]
-                nc.scalar.activation(y[:, lo:hi], acc[:, lo:hi], IDENTITY, bias=column)
-            return y
-
-        def scatter(c, i, y):
-            lo, hi = CHUNKS[c]
-            if c == 0:
-                windows[i] = held.tile([P, T], F32, name=f"window{i}", tag=f"window{i}", align_bytes=64)
-            nc.vector.tensor_tensor(windows[i][:].indirect(columns(dst_t, c)), y[:], gate_t[:, lo:hi], MULT)
-            if c == len(CHUNKS) - 1:
+        def product(e, i, lo, hi, bank, column, slot):
+            acc = psum.tile([P, 512], F32, name="acc", tag=f"bank{bank}")
+            nc.tensor.matmul_mx(
+                out=acc[:, 0 : hi - lo],
+                lhsT=words[:, e, 2 * P * i : 2 * P * (i + 1)].bitcast(FP4X4),
+                lhsT_scale=ws[min(e, 1)][:, e - min(e, 1), P * i : P * (i + 1)],
+                rhs=codes[e][:, lo:hi].bitcast(FP8X4),
+                rhs_scale=scales[e][:, lo:hi],
+                start=True,
+                stop=True,
+            )
+            y = tile([P, hi - lo], F32, f"y{e}_{i}_{lo}", slot)
+            nc.scalar.activation(y[:], acc[:, 0 : hi - lo], IDENTITY, bias=column)
+            lo, hi = C * e + lo, C * e + hi
+            nc.vector.tensor_tensor(windows[i][:].indirect(entries(dst_t, lo, hi)), y[:], gate_t[:, lo:hi], MULT)
+            if e == E - 1:
                 nc.sync.dma_start(out=out[P * i : P * (i + 1), :], in_=windows[i][:])
 
-        def gather(c, grouped, j):
-            for part, (e, lo, hi) in zip(grouped, expert_runs(c)):
-                picks = offs_t[:, (CHUNKS[c][0] + lo) // 16 : (CHUNKS[c][0] + hi) // 16]
-                nc.scalar.activation(part[:, :, j], halves[j][:].indirect(picks), COPY)
+        def pick(into, e, j):
+            nc.scalar.activation(into, halves[j][:].indirect(entries(offs_t, C * e, C * (e + 1))), COPY)
 
-        def grouped_tile(c):
-            return held.tile([P, CHUNKS[c][1] - CHUNKS[c][0], PACK], BF16, name=f"grouped{c}", align_bytes=64)
-
-        def gather_then_interleave(c):
-            n = CHUNKS[c][1] - CHUNKS[c][0]
-            picked = held.tile([P, PACK, n], BF16, name=f"picked{c}", tag=f"picked{c}", align_bytes=64)
-            for j in range(PACK):
-                nc.scalar.activation(picked[:, j, :], halves[j][:].indirect(columns(offs_t, c)), COPY)
-            woven = grouped_tile(c)
+        def pick_and_weave(e, woven, first):
+            picked = tile([P, PACK - first, C], BF16, f"picked{e}")
+            for j in range(first, PACK):
+                pick(picked[:, j - first, :], e, j)
             nc.scalar.copy(
-                woven[:].rearrange("p (s u) j -> p s j u", u=4), picked[:].rearrange("p j (s u) -> p s j u", u=4)
+                woven[:, :, first:PACK].rearrange("p (s u) j -> p s j u", u=4),
+                picked[:].rearrange("p j (s u) -> p s j u", u=4),
             )
-            return [woven]
 
-        grouped0 = held.tile([P, first, PACK], BF16, name="grouped0", align_bytes=64)
-        grouped = [
-            held.tile([P, hi - lo, PACK], BF16, name=f"second{e}", tag=f"window{2 + e}", align_bytes=64)
-            for e, lo, hi in expert_runs(1)
-        ]
-        halves = []
+        woven0 = tile([P, C, PACK], BF16, "woven0")
+        woven = tile([P, C, PACK], BF16, "woven1")
+        codes[0] = tile([P, C], U32, "codes0")
         for j in range(PACK - 1):
-            halves.append(held.tile([P, T], BF16, name=f"half{j}"))
-            nc.vector.tensor_copy(halves[j][:], planes[j][:])
-            nc.vector.tensor_copy(grouped0[:, :, j], planes[j][:].indirect(columns(offs_t, 0)))
-            gather(1, grouped, j)
-        nc.vector.tensor_copy(grouped0[:, :, 3], planes[3][:].indirect(columns(offs_t, 0)))
-        quantize(0, [grouped0])
-        halves.append(held.tile([P, T], BF16, name="half3", tag="late", align_bytes=64))
-        nc.vector.tensor_copy(halves[3][:], planes[3][:])
-        for c in range(len(CHUNKS)):
-            for i in (0, 1):
-                scatter(c, i, product(c, i))
-            if c + 1 < len(CHUNKS):
-                if c > 0:
-                    grouped = gather_then_interleave(c + 1)
-                else:
-                    gather(1, grouped, 3)
-                quantize(c + 1, grouped)
-            for i in (2, 3):
-                scatter(c, i, product(c, i))
+            nc.vector.tensor_copy(woven0[:, :, j], planes[j][:].indirect(entries(offs_t, 0, C)))
+            nc.gpsimd.tensor_scalar(halves[j][:], planes[j][:], 1.0, 0.0, op0=MULT, op1=ADD)
+            pick(woven[:, :, j], 1, j)
+        for h in range(2):
+            lo, hi = HALF * h, HALF * (h + 1)
+            nc.vector.tensor_copy(woven0[:, lo:hi, 3], planes[3][:].indirect(entries(offs_t, lo, hi)))
+            quantize(0, woven0, lo, hi)
+            nc.vector.tensor_copy(halves[3][:, T // 2 * h : T // 2 * (h + 1)], planes[3][:, T // 2 * h : T // 2 * (h + 1)])
+        for h, columns in enumerate((opening_bias, early[0])):
+            for i in range(2):
+                product(0, i, HALF * h, HALF * (h + 1), 2 * h + i, columns[:, i, :], "codes1" if (h, i) == (1, 0) else None)
+        for e in range(E):
+            if e > 0:
+                for i in range(2):
+                    product(e, i, 0, C, i, early[e][:, i, :], f"codes{e + 1}" if i == 0 else None)
+            if e + 1 < E:
+                if e > 0:
+                    woven = tile([P, C, PACK], BF16, f"woven{e + 1}")
+                pick_and_weave(e + 1, woven, 0 if e else PACK - 1)
+                codes[e + 1] = tile([P, C], U32, f"codes{e + 1}")
+                quantize(e + 1, woven, 0, C)
+            for i in range(2, N_TILES):
+                product(e, i, 0, C, 2, late[:, i - 2, e : e + 1], f"picked{e + 1}" if i == 2 else None)

@@ -62,12 +62,12 @@ def tile_moe_two_lin_bias_kernel(tc, xT, w_words, w_scales, b, gate, offs, dst, 
         nc.sync.dma_start(out=planes[0][:], in_=x_rows[:, 0, :])
         nc.sync.dma_start(offs_t[:], offs)
         nc.sync.dma_start(dst_t[:], dst)
-        load_bias(opening_bias, 0)
         for j in range(1, PACK):
             nc.sync.dma_start(out=planes[j][:], in_=x_rows[:, j, :])
         nc.sync.dma_start(out=words[:, 0:1].bitcast(I32), in_=word_rows[:, 0:1])
-        load_scales(0)
         nc.sync.dma_start(out=gate_t[:, 0:C], in_=gate[0:P, 0:C])
+        load_scales(0)
+        load_bias(opening_bias, 0)
         load_bias(early[0], 0)
         nc.sync.dma_start(out=late[:], in_=bias_rows[:, 2:4, :])
         nc.sync.dma_start(out=words[:, 1:E].bitcast(I32), in_=word_rows[:, 1:E])

@@ -6,6 +6,7 @@ K, T, E, C, N = 512, 1024, 4, 256, 512
 P = 128
 PACK = 4
 N_TILES = N // P
+BANK = 512
 
 FLOPS = 2 * K * N * E * C
 BYTES = 4 * (K * T + N * E + E * C + N * T) + E * (K * N // 2 + K // 32 * N) + 2 * 2 * P * (T // 16)
@@ -22,7 +23,10 @@ COPY = mybir.ActivationFunctionType.Copy
 IDENTITY = mybir.ActivationFunctionType.Identity
 MULT = mybir.AluOpType.mult
 ADD = mybir.AluOpType.add
-HALF = C // 2
+
+FIRST = (0, 128)
+MIDDLE = (128, 512)
+LAST = (512, 1024)
 
 
 def tile_moe_two_lin_bias_kernel(tc, xT, w_words, w_scales, b, gate, offs, dst, out):
@@ -39,113 +43,123 @@ def tile_moe_two_lin_bias_kernel(tc, xT, w_words, w_scales, b, gate, offs, dst, 
         x_rows = xT.rearrange("(p j) w -> p j w", j=PACK)
         planes = [tile([P, T], F32, f"plane{j}") for j in range(PACK)]
         word_rows = w_words.rearrange("e a p n -> p (e a) n").bitcast(I32)
-        words = tile([P, E, 2 * N], U8, "words")
+        words = [tile([P, 2 * N], U8, "words0"), tile([P, E - 1, 2 * N], U8, "words_rest")]
         scale_rows = w_scales.rearrange("e a (q r) n -> r (a q) e n", r=4).bitcast(I32)
-        groups = ((0, 1), (1, E))
-        ws = [tile([P, z - a, N], U8, f"ws{a}") for a, z in groups]
-        bias_rows = b.rearrange("(i p) e -> p i e", p=P)
-        opening_bias = tile([P, 2, 1], F32, "opening_bias", "picked1")
-        early = [tile([P, 2, 1], F32, f"early{e}", f"picked{e + 1}" if e else None) for e in range(E)]
-        late = tile([P, 2, E], F32, "late_bias")
+        w_scale = tile([P, E, N], U8, "w_scale")
+        bias = tile([P, N_TILES, E], F32, "bias")
         gate_t = tile([P, E * C], F32, "gate_t")
 
-        def load_bias(columns, e):
-            with nc.allow_non_contiguous_dma(reason="one bias value for each output channel"):
-                nc.sync.dma_start(out=columns[:], in_=bias_rows[:, 0:2, e : e + 1])
-
-        def load_scales(group):
-            for r in range(4):
-                nc.sync.dma_start(out=ws[group][r:P:32].bitcast(I32), in_=scale_rows[r][:, groups[group][0] : groups[group][1]])
-
-        for group in range(2):
-            nc.vector.memset(ws[group][:].bitcast(I32), 0)
-        nc.sync.dma_start(out=planes[0][:], in_=x_rows[:, 0, :])
+        nc.vector.memset(w_scale[:].bitcast(I32), 0)
         nc.sync.dma_start(offs_t[:], offs)
+        nc.sync.dma_start(out=planes[0][:], in_=x_rows[:, 0, :])
         nc.sync.dma_start(dst_t[:], dst)
         for j in range(1, PACK):
             nc.sync.dma_start(out=planes[j][:], in_=x_rows[:, j, :])
-        nc.sync.dma_start(out=words[:, 0:1].bitcast(I32), in_=word_rows[:, 0:1])
-        nc.sync.dma_start(out=gate_t[:, 0:C], in_=gate[0:P, 0:C])
-        load_scales(0)
-        load_bias(opening_bias, 0)
-        load_bias(early[0], 0)
-        nc.sync.dma_start(out=late[:], in_=bias_rows[:, 2:4, :])
-        nc.sync.dma_start(out=words[:, 1:E].bitcast(I32), in_=word_rows[:, 1:E])
-        load_scales(1)
-        load_bias(early[1], 1)
-        nc.sync.dma_start(out=gate_t[:, C : E * C], in_=gate[0:P, C : E * C])
-        for e in range(2, E):
-            load_bias(early[e], e)
+        nc.sync.dma_start(out=words[0][:].bitcast(I32), in_=word_rows[:, 0])
+        nc.sync.dma_start(out=gate_t[:, FIRST[0] : FIRST[1]], in_=gate[0:P, FIRST[0] : FIRST[1]])
+        for r in range(4):
+            nc.sync.dma_start(out=w_scale[r:P:32].bitcast(I32), in_=scale_rows[r])
+        nc.sync.dma_start(out=bias[:], in_=b.rearrange("(i p) e -> p i e", p=P))
+        nc.sync.dma_start(out=words[1][:].bitcast(I32), in_=word_rows[:, 1:E])
+        nc.sync.dma_start(out=gate_t[:, FIRST[1] : T], in_=gate[0:P, FIRST[1] : T])
 
-        halves = [tile([P, T], BF16, f"half{j}") for j in range(PACK)]
         windows = [tile([P, T], F32, f"window{i}") for i in range(N_TILES)]
-        scales = [tile([P, C], U8, f"scales{e}") for e in range(E)]
-        codes = {}
+        sums = [tile([P, T], F32, f"sums{i}") for i in range(N_TILES)]
+        banks = [[psum.tile([P, BANK], F32, name=f"bank{i}_{h}") for h in range(2)] for i in range(N_TILES)]
+        woven, codes, scales = {}, {}, {}
 
         def entries(listed, lo, hi):
             return listed[:, lo // 16 : hi // 16]
 
-        def quantize(e, woven, lo, hi):
+        def tokens(j, lo, hi):
+            return planes[j][:].indirect(entries(offs_t, lo, hi))
+
+        def weave(copy, into, picked):
+            copy(into.rearrange("p (s u) j -> p s j u", u=4), picked.rearrange("p j (s u) -> p s j u", u=4))
+
+        def quantize(chunk):
+            width = chunk[1] - chunk[0]
+            codes[chunk] = tile([P, width], U32, f"codes{chunk[0]}")
+            scales[chunk] = tile([P, width], U8, f"scales{chunk[0]}")
             nc.vector.quantize_mx(
-                out=codes[e][:, lo:hi].bitcast(FP8X4),
-                scales=scales[e][:, lo:hi],
-                in_=woven[:, lo:hi, :].rearrange("p w j -> p (w j)"),
+                out=codes[chunk][:].bitcast(FP8X4),
+                scales=scales[chunk][:],
+                in_=woven[chunk][:].rearrange("p w j -> p (w j)"),
             )
 
-        def product(e, i, lo, hi, bank, column, slot):
-            acc = psum.tile([P, 512], F32, name="acc", tag=f"bank{bank}")
-            nc.tensor.matmul_mx(
-                out=acc[:, 0 : hi - lo],
-                lhsT=words[:, e, 2 * P * i : 2 * P * (i + 1)].bitcast(FP4X4),
-                lhsT_scale=ws[min(e, 1)][:, e - min(e, 1), P * i : P * (i + 1)],
-                rhs=codes[e][:, lo:hi].bitcast(FP8X4),
-                rhs_scale=scales[e][:, lo:hi],
-                start=True,
-                stop=True,
-            )
-            y = tile([P, hi - lo], F32, f"y{e}_{i}_{lo}", slot)
-            nc.scalar.activation(y[:], acc[:, 0 : hi - lo], IDENTITY, bias=column)
-            lo, hi = C * e + lo, C * e + hi
-            nc.vector.tensor_tensor(windows[i][:].indirect(entries(dst_t, lo, hi)), y[:], gate_t[:, lo:hi], MULT)
-            if e == E - 1:
-                nc.sync.dma_start(out=out[P * i : P * (i + 1), :], in_=windows[i][:])
+        def by_expert(lo, hi):
+            return [(e, max(lo, C * e), min(hi, C * (e + 1))) for e in range(lo // C, (hi - 1) // C + 1)]
 
-        def pick(into, e, j):
-            nc.scalar.activation(into, halves[j][:].indirect(entries(offs_t, C * e, C * (e + 1))), COPY)
+        def in_bank(i, lo, hi):
+            return banks[i][lo // BANK][:, lo % BANK : lo % BANK + hi - lo]
 
-        def pick_and_weave(e, woven, first):
-            picked = tile([P, PACK - first, C], BF16, f"picked{e}")
-            for j in range(first, PACK):
-                pick(picked[:, j - first, :], e, j)
-            nc.scalar.copy(
-                woven[:, :, first:PACK].rearrange("p (s u) j -> p s j u", u=4),
-                picked[:].rearrange("p j (s u) -> p s j u", u=4),
-            )
+        def products(chunk):
+            for i in range(N_TILES):
+                for e, lo, hi in by_expert(*chunk):
+                    columns = slice(2 * P * i, 2 * P * (i + 1))
+                    nc.tensor.matmul_mx(
+                        out=in_bank(i, lo, hi),
+                        lhsT=(words[1][:, e - 1, columns] if e else words[0][:, columns]).bitcast(FP4X4),
+                        lhsT_scale=w_scale[:, e, P * i : P * (i + 1)],
+                        rhs=codes[chunk][:, lo - chunk[0] : hi - chunk[0]].bitcast(FP8X4),
+                        rhs_scale=scales[chunk][:, lo - chunk[0] : hi - chunk[0]],
+                        start=True,
+                        stop=True,
+                    )
 
-        woven0 = tile([P, C, PACK], BF16, "woven0")
-        woven = tile([P, C, PACK], BF16, "woven1")
-        codes[0] = tile([P, C], U32, "codes0")
-        for j in range(PACK - 1):
-            nc.vector.tensor_copy(woven0[:, :, j], planes[j][:].indirect(entries(offs_t, 0, C)))
-            nc.gpsimd.tensor_scalar(halves[j][:], planes[j][:], 1.0, 0.0, op0=MULT, op1=ADD)
-            pick(woven[:, :, j], 1, j)
-        for h in range(2):
-            lo, hi = HALF * h, HALF * (h + 1)
-            nc.vector.tensor_copy(woven0[:, lo:hi, 3], planes[3][:].indirect(entries(offs_t, lo, hi)))
-            quantize(0, woven0, lo, hi)
-            nc.vector.tensor_copy(halves[3][:, T // 2 * h : T // 2 * (h + 1)], planes[3][:, T // 2 * h : T // 2 * (h + 1)])
-        for h, columns in enumerate((opening_bias, early[0])):
-            for i in range(2):
-                product(0, i, HALF * h, HALF * (h + 1), 2 * h + i, columns[:, i, :], "codes1" if (h, i) == (1, 0) else None)
-        for e in range(E):
-            if e > 0:
-                for i in range(2):
-                    product(e, i, 0, C, i, early[e][:, i, :], f"codes{e + 1}" if i == 0 else None)
-            if e + 1 < E:
-                if e > 0:
-                    woven = tile([P, C, PACK], BF16, f"woven{e + 1}")
-                pick_and_weave(e + 1, woven, 0 if e else PACK - 1)
-                codes[e + 1] = tile([P, C], U32, f"codes{e + 1}")
-                quantize(e + 1, woven, 0, C)
-            for i in range(2, N_TILES):
-                product(e, i, 0, C, 2, late[:, i - 2, e : e + 1], f"picked{e + 1}" if i == 2 else None)
+        def gated(i, lo, hi):
+            for e, a, z in by_expert(lo, hi):
+                nc.vector.scalar_tensor_tensor(sums[i][:, a:z], in_bank(i, a, z), bias[:, i, e : e + 1], gate_t[:, a:z], ADD, MULT)
+
+        def biased(i, lo, hi):
+            for e, a, z in by_expert(lo, hi):
+                nc.scalar.activation(sums[i][:, a:z], in_bank(i, a, z), IDENTITY, bias=bias[:, i, e : e + 1])
+
+        def scalar_scatter(i, lo, hi):
+            nc.scalar.activation(windows[i][:].indirect(entries(dst_t, lo, hi)), sums[i][:, lo:hi], COPY)
+
+        def vector_scatter(i, lo, hi):
+            nc.vector.tensor_tensor(windows[i][:].indirect(entries(dst_t, lo, hi)), sums[i][:, lo:hi], gate_t[:, lo:hi], MULT)
+
+        def store(i):
+            nc.sync.dma_start(out=out[P * i : P * (i + 1), :], in_=windows[i][:])
+
+        woven[FIRST] = tile([P, 128, PACK], BF16, "woven_first")
+        picked_middle = tile([P, PACK, 384], BF16, "picked_middle")
+        picked_last = tile([P, PACK, 512], BF16, "picked_last")
+        for j in range(PACK):
+            nc.vector.tensor_copy(woven[FIRST][:, :, j], tokens(j, *FIRST))
+            nc.scalar.activation(picked_last[:, j, :], tokens(j, *LAST), COPY)
+            if j < PACK - 1:
+                nc.vector.tensor_copy(picked_middle[:, j, :], tokens(j, *MIDDLE))
+        nc.vector.tensor_copy(picked_middle[:, 3, 0:128], tokens(3, 128, 256))
+        quantize(FIRST)
+        products(FIRST)
+        nc.vector.tensor_copy(picked_middle[:, 3, 128:384], tokens(3, 256, 512))
+        woven[LAST] = tile([P, 512, PACK], BF16, "woven_last")
+        weave(nc.scalar.copy, woven[LAST][:, 0:C, :], picked_last[:, :, 0:C])
+        weave(nc.vector.tensor_copy, woven[LAST][:, C : 2 * C, :], picked_last[:, :, C : 2 * C])
+        for i in range(3):
+            gated(i, *FIRST)
+            scalar_scatter(i, *FIRST)
+        biased(3, *FIRST)
+        woven[MIDDLE] = tile([P, 384, PACK], BF16, "woven_middle", "codes0")
+        weave(nc.vector.tensor_copy, woven[MIDDLE][:], picked_middle[:])
+        quantize(LAST)
+        products(LAST)
+        quantize(MIDDLE)
+        products(MIDDLE)
+        for scalar_window, vector_window in ((0, 3), (1, 2)):
+            gated(scalar_window, *LAST)
+            biased(vector_window, *LAST)
+            if vector_window == 3:
+                vector_scatter(3, *FIRST)
+            scalar_scatter(scalar_window, 512, 768)
+            gated(scalar_window, *MIDDLE)
+            biased(vector_window, *MIDDLE)
+            vector_scatter(vector_window, *LAST)
+            scalar_scatter(scalar_window, 768, 1024)
+            scalar_scatter(scalar_window, *MIDDLE)
+            vector_scatter(vector_window, *MIDDLE)
+            store(scalar_window)
+            store(vector_window)

@@ -24,8 +24,8 @@ IDENTITY = mybir.ActivationFunctionType.Identity
 MULT = mybir.AluOpType.mult
 ADD = mybir.AluOpType.add
 
-FIRST = (0, 128)
-MIDDLE = (128, 512)
+FIRST = (0, 256)
+MIDDLE = (256, 512)
 LAST = (512, 1024)
 
 
@@ -34,6 +34,7 @@ def tile_moe_two_lin_bias_kernel(tc, xT, w_words, w_scales, b, gate, offs, dst, 
     with ExitStack() as ctx:
         held = ctx.enter_context(tc.tile_pool(name="held", bufs=1))
         psum = ctx.enter_context(tc.psum_pool(name="psum", bufs=1))
+        laid = ctx.enter_context(tc.tile_pool(name="laid", bufs=1))
 
         def tile(shape, dtype, name, slot=None):
             return held.tile(shape, dtype, name=name, tag=slot or name, align_bytes=64)
@@ -47,19 +48,23 @@ def tile_moe_two_lin_bias_kernel(tc, xT, w_words, w_scales, b, gate, offs, dst, 
         scale_rows = w_scales.rearrange("e a (q r) n -> r (a q) e n", r=4).bitcast(I32)
         w_scale = tile([P, E, N], U8, "w_scale")
         bias = tile([P, N_TILES, E], F32, "bias")
+        gate_first = laid.tile([P, C], F32, name="gate_first", offset=3584, align_bytes=64)
         gate_t = tile([P, E * C], F32, "gate_t")
 
+        warm = tile([P, 16], F32, "warm")
+        nc.gpsimd.memset(warm[:, 0:1], 0.0)
+        nc.scalar.activation(warm[:, 8:9], warm[:, 0:1], COPY)
         nc.vector.memset(w_scale[:].bitcast(I32), 0)
-        nc.sync.dma_start(offs_t[:], offs)
         nc.sync.dma_start(out=planes[0][:], in_=x_rows[:, 0, :])
+        nc.sync.dma_start(offs_t[:], offs)
         nc.sync.dma_start(dst_t[:], dst)
         for j in range(1, PACK):
             nc.sync.dma_start(out=planes[j][:], in_=x_rows[:, j, :])
         nc.sync.dma_start(out=words[0][:].bitcast(I32), in_=word_rows[:, 0])
-        nc.sync.dma_start(out=gate_t[:, FIRST[0] : FIRST[1]], in_=gate[0:P, FIRST[0] : FIRST[1]])
+        nc.sync.dma_start(out=bias[:], in_=b.rearrange("(i p) e -> p i e", p=P))
         for r in range(4):
             nc.sync.dma_start(out=w_scale[r:P:32].bitcast(I32), in_=scale_rows[r])
-        nc.sync.dma_start(out=bias[:], in_=b.rearrange("(i p) e -> p i e", p=P))
+        nc.sync.dma_start(out=gate_first[:], in_=gate[0:P, FIRST[0] : FIRST[1]])
         nc.sync.dma_start(out=words[1][:].bitcast(I32), in_=word_rows[:, 1:E])
         nc.sync.dma_start(out=gate_t[:, FIRST[1] : T], in_=gate[0:P, FIRST[1] : T])
 
@@ -79,7 +84,10 @@ def tile_moe_two_lin_bias_kernel(tc, xT, w_words, w_scales, b, gate, offs, dst, 
 
         def quantize(chunk):
             width = chunk[1] - chunk[0]
-            codes[chunk] = tile([P, width], U32, f"codes{chunk[0]}")
+            if chunk == MIDDLE:
+                codes[chunk] = laid.tile([P, width], U32, name="codes_middle", offset=4096, align_bytes=64)
+            else:
+                codes[chunk] = tile([P, width], U32, f"codes{chunk[0]}")
             scales[chunk] = tile([P, width], U8, f"scales{chunk[0]}")
             nc.vector.quantize_mx(
                 out=codes[chunk][:].bitcast(FP8X4),
@@ -109,7 +117,7 @@ def tile_moe_two_lin_bias_kernel(tc, xT, w_words, w_scales, b, gate, offs, dst, 
 
         def gated(i, lo, hi):
             for e, a, z in by_expert(lo, hi):
-                nc.vector.scalar_tensor_tensor(sums[i][:, a:z], in_bank(i, a, z), bias[:, i, e : e + 1], gate_t[:, a:z], ADD, MULT)
+                nc.vector.scalar_tensor_tensor(sums[i][:, a:z], in_bank(i, a, z), bias[:, i, e : e + 1], (gate_t if a else gate_first)[:, a:z], ADD, MULT)
 
         def biased(i, lo, hi):
             for e, a, z in by_expert(lo, hi):
@@ -124,42 +132,47 @@ def tile_moe_two_lin_bias_kernel(tc, xT, w_words, w_scales, b, gate, offs, dst, 
         def store(i):
             nc.sync.dma_start(out=out[P * i : P * (i + 1), :], in_=windows[i][:])
 
-        woven[FIRST] = tile([P, 128, PACK], BF16, "woven_first")
-        picked_middle = tile([P, PACK, 384], BF16, "picked_middle")
-        picked_last = tile([P, PACK, 512], BF16, "picked_last")
+        woven[FIRST] = tile([P, C, PACK], BF16, "woven_first")
+        picked_middle = tile([P, PACK, C], BF16, "picked_middle")
+        picked_last = tile([P, PACK, 2 * C], BF16, "picked_last")
         for j in range(PACK):
             nc.vector.tensor_copy(woven[FIRST][:, :, j], tokens(j, *FIRST))
+            share = (C, C, 0, C // 2)[j]
+            if share:
+                nc.vector.tensor_copy(picked_middle[:, j, 0:share], tokens(j, C, C + share))
+            if share < C:
+                nc.scalar.activation(picked_middle[:, j, share:C], tokens(j, C + share, 2 * C), COPY)
             nc.scalar.activation(picked_last[:, j, :], tokens(j, *LAST), COPY)
-            if j < PACK - 1:
-                nc.vector.tensor_copy(picked_middle[:, j, :], tokens(j, *MIDDLE))
-        nc.vector.tensor_copy(picked_middle[:, 3, 0:128], tokens(3, 128, 256))
         quantize(FIRST)
         products(FIRST)
-        nc.vector.tensor_copy(picked_middle[:, 3, 128:384], tokens(3, 256, 512))
-        woven[LAST] = tile([P, 512, PACK], BF16, "woven_last")
-        weave(nc.scalar.copy, woven[LAST][:, 0:C, :], picked_last[:, :, 0:C])
-        weave(nc.vector.tensor_copy, woven[LAST][:, C : 2 * C, :], picked_last[:, :, C : 2 * C])
-        for i in range(3):
-            gated(i, *FIRST)
-            scalar_scatter(i, *FIRST)
-        biased(3, *FIRST)
-        woven[MIDDLE] = tile([P, 384, PACK], BF16, "woven_middle", "codes0")
+        woven[MIDDLE] = tile([P, C, PACK], BF16, "woven_middle")
         weave(nc.vector.tensor_copy, woven[MIDDLE][:], picked_middle[:])
-        quantize(LAST)
-        products(LAST)
+        for i in range(N_TILES):
+            gated(i, *FIRST)
+        for i in range(3):
+            scalar_scatter(i, *FIRST)
         quantize(MIDDLE)
         products(MIDDLE)
+        woven[LAST] = laid.tile([P, 2 * C, PACK], BF16, name="woven_last", offset=0, align_bytes=64)
+        weave(nc.vector.tensor_copy, woven[LAST][:], picked_last[:])
+        gated(0, *MIDDLE)
+        quantize(LAST)
+        products(LAST)
+        for i in (3, 2):
+            biased(i, *MIDDLE)
+        scalar_scatter(0, *MIDDLE)
+        gated(1, *MIDDLE)
+        gated(0, *LAST)
+        for i in (3, 2):
+            biased(i, *LAST)
+        nc.vector.tensor_copy(windows[3][:].indirect(entries(dst_t, *FIRST)), sums[3][:, FIRST[0] : FIRST[1]])
+        gated(1, *LAST)
         for scalar_window, vector_window in ((0, 3), (1, 2)):
-            gated(scalar_window, *LAST)
-            biased(vector_window, *LAST)
-            if vector_window == 3:
-                vector_scatter(3, *FIRST)
-            scalar_scatter(scalar_window, 512, 768)
-            gated(scalar_window, *MIDDLE)
-            biased(vector_window, *MIDDLE)
-            vector_scatter(vector_window, *LAST)
-            scalar_scatter(scalar_window, 768, 1024)
-            scalar_scatter(scalar_window, *MIDDLE)
+            if scalar_window:
+                scalar_scatter(scalar_window, *MIDDLE)
             vector_scatter(vector_window, *MIDDLE)
+            scalar_scatter(scalar_window, 512, 768)
+            scalar_scatter(scalar_window, 768, 1024)
+            vector_scatter(vector_window, *LAST)
             store(scalar_window)
             store(vector_window)

@@ -20,13 +20,10 @@ U8 = mybir.dt.uint8
 FP8X4 = mybir.dt.float8_e4m3fn_x4
 FP4X4 = mybir.dt.float4_e2m1fn_x4
 COPY = mybir.ActivationFunctionType.Copy
-IDENTITY = mybir.ActivationFunctionType.Identity
 MULT = mybir.AluOpType.mult
 ADD = mybir.AluOpType.add
 
-FIRST = (0, 256)
-MIDDLE = (256, 512)
-LAST = (512, 1024)
+HALF = C // 2
 
 
 def tile_moe_two_lin_bias_kernel(tc, xT, w_words, w_scales, b, gate, offs, dst, out):
@@ -34,7 +31,6 @@ def tile_moe_two_lin_bias_kernel(tc, xT, w_words, w_scales, b, gate, offs, dst, 
     with ExitStack() as ctx:
         held = ctx.enter_context(tc.tile_pool(name="held", bufs=1))
         psum = ctx.enter_context(tc.psum_pool(name="psum", bufs=1))
-        laid = ctx.enter_context(tc.tile_pool(name="laid", bufs=1))
 
         def tile(shape, dtype, name, slot=None):
             return held.tile(shape, dtype, name=name, tag=slot or name, align_bytes=64)
@@ -48,8 +44,7 @@ def tile_moe_two_lin_bias_kernel(tc, xT, w_words, w_scales, b, gate, offs, dst, 
         scale_rows = w_scales.rearrange("e a (q r) n -> r (a q) e n", r=4).bitcast(I32)
         w_scale = tile([P, E, N], U8, "w_scale")
         bias = tile([P, N_TILES, E], F32, "bias")
-        gate_first = laid.tile([P, C], F32, name="gate_first", offset=3584, align_bytes=64)
-        gate_t = tile([P, E * C], F32, "gate_t")
+        gates = [tile([P, C], F32, "gate0", "codes1"), tile([P, T - C], F32, "gate_rest")]
 
         warm = tile([P, 16], F32, "warm")
         nc.gpsimd.memset(warm[:, 0:1], 0.0)
@@ -64,14 +59,14 @@ def tile_moe_two_lin_bias_kernel(tc, xT, w_words, w_scales, b, gate, offs, dst, 
         nc.sync.dma_start(out=bias[:], in_=b.rearrange("(i p) e -> p i e", p=P))
         for r in range(4):
             nc.sync.dma_start(out=w_scale[r:P:32].bitcast(I32), in_=scale_rows[r])
-        nc.sync.dma_start(out=gate_first[:], in_=gate[0:P, FIRST[0] : FIRST[1]])
+        nc.sync.dma_start(out=gates[0][:], in_=gate[0:P, 0:C])
         nc.sync.dma_start(out=words[1][:].bitcast(I32), in_=word_rows[:, 1:E])
-        nc.sync.dma_start(out=gate_t[:, FIRST[1] : T], in_=gate[0:P, FIRST[1] : T])
+        nc.sync.dma_start(out=gates[1][:], in_=gate[0:P, C:T])
 
         windows = [tile([P, T], F32, f"window{i}") for i in range(N_TILES)]
         sums = [tile([P, T], F32, f"sums{i}") for i in range(N_TILES)]
-        banks = [[psum.tile([P, BANK], F32, name=f"bank{i}_{h}") for h in range(2)] for i in range(N_TILES)]
-        woven, codes, scales = {}, {}, {}
+        codes = {0: tile([P, C], U32, "codes0")}
+        scales = [tile([P, C], U8, f"scales{e}") for e in range(E)]
 
         def entries(listed, lo, hi):
             return listed[:, lo // 16 : hi // 16]
@@ -79,100 +74,103 @@ def tile_moe_two_lin_bias_kernel(tc, xT, w_words, w_scales, b, gate, offs, dst, 
         def tokens(j, lo, hi):
             return planes[j][:].indirect(entries(offs_t, lo, hi))
 
-        def weave(copy, into, picked):
-            copy(into.rearrange("p (s u) j -> p s j u", u=4), picked.rearrange("p j (s u) -> p s j u", u=4))
+        def weave(into, picked):
+            nc.gpsimd.tensor_scalar(into, picked.rearrange("p j w -> p w j"), 1.0, 0.0, op0=MULT, op1=ADD)
 
-        def quantize(chunk):
-            width = chunk[1] - chunk[0]
-            if chunk == MIDDLE:
-                codes[chunk] = laid.tile([P, width], U32, name="codes_middle", offset=4096, align_bytes=64)
-            else:
-                codes[chunk] = tile([P, width], U32, f"codes{chunk[0]}")
-            scales[chunk] = tile([P, width], U8, f"scales{chunk[0]}")
+        def quantize(e, woven, lo=0, hi=C):
             nc.vector.quantize_mx(
-                out=codes[chunk][:].bitcast(FP8X4),
-                scales=scales[chunk][:],
-                in_=woven[chunk][:].rearrange("p w j -> p (w j)"),
+                out=codes[e][:, lo:hi].bitcast(FP8X4),
+                scales=scales[e][:, lo:hi],
+                in_=woven[:, lo:hi, :].rearrange("p w j -> p (w j)"),
             )
 
-        def by_expert(lo, hi):
-            return [(e, max(lo, C * e), min(hi, C * (e + 1))) for e in range(lo // C, (hi - 1) // C + 1)]
+        banks = [[psum.tile([P, 2, C], F32, name=f"bank{i}_{h}") for h in range(2)] for i in range(N_TILES)]
 
-        def in_bank(i, lo, hi):
-            return banks[i][lo // BANK][:, lo % BANK : lo % BANK + hi - lo]
+        def product(i, e, lo=0, hi=C, acc=None):
+            acc = banks[i][e // 2][:, e % 2, :] if acc is None else acc
+            columns = slice(2 * P * i, 2 * P * (i + 1))
+            nc.tensor.matmul_mx(
+                out=acc[:, lo:hi],
+                lhsT=(words[1][:, e - 1, columns] if e else words[0][:, columns]).bitcast(FP4X4),
+                lhsT_scale=w_scale[:, e, P * i : P * (i + 1)],
+                rhs=codes[e][:, lo:hi].bitcast(FP8X4),
+                rhs_scale=scales[e][:, lo:hi],
+                start=True,
+                stop=True,
+            )
+            return acc
 
-        def products(chunk):
-            for i in range(N_TILES):
-                for e, lo, hi in by_expert(*chunk):
-                    columns = slice(2 * P * i, 2 * P * (i + 1))
-                    nc.tensor.matmul_mx(
-                        out=in_bank(i, lo, hi),
-                        lhsT=(words[1][:, e - 1, columns] if e else words[0][:, columns]).bitcast(FP4X4),
-                        lhsT_scale=w_scale[:, e, P * i : P * (i + 1)],
-                        rhs=codes[chunk][:, lo - chunk[0] : hi - chunk[0]].bitcast(FP8X4),
-                        rhs_scale=scales[chunk][:, lo - chunk[0] : hi - chunk[0]],
-                        start=True,
-                        stop=True,
-                    )
+        def gate_of(e):
+            return gates[1][:, C * (e - 1) : C * e] if e else gates[0]
 
-        def gated(i, lo, hi):
-            for e, a, z in by_expert(lo, hi):
-                nc.vector.scalar_tensor_tensor(sums[i][:, a:z], in_bank(i, a, z), bias[:, i, e : e + 1], (gate_t if a else gate_first)[:, a:z], ADD, MULT)
-
-        def biased(i, lo, hi):
-            for e, a, z in by_expert(lo, hi):
-                nc.scalar.activation(sums[i][:, a:z], in_bank(i, a, z), IDENTITY, bias=bias[:, i, e : e + 1])
+        def gated(acc, i, e, lo=0, hi=C):
+            slots = slice(C * e + lo, C * e + hi)
+            nc.vector.scalar_tensor_tensor(sums[i][:, slots], acc[:, lo:hi], bias[:, i, e : e + 1], gate_of(e)[:, lo:hi], ADD, MULT)
 
         def scalar_scatter(i, lo, hi):
             nc.scalar.activation(windows[i][:].indirect(entries(dst_t, lo, hi)), sums[i][:, lo:hi], COPY)
 
         def vector_scatter(i, lo, hi):
-            nc.vector.tensor_tensor(windows[i][:].indirect(entries(dst_t, lo, hi)), sums[i][:, lo:hi], gate_t[:, lo:hi], MULT)
+            nc.vector.tensor_copy(windows[i][:].indirect(entries(dst_t, lo, hi)), sums[i][:, lo:hi])
 
         def store(i):
-            nc.sync.dma_start(out=out[P * i : P * (i + 1), :], in_=windows[i][:])
+            (nc.scalar if i < 2 else nc.sync).dma_start(out=out[P * i : P * (i + 1), :], in_=windows[i][:])
 
-        woven[FIRST] = tile([P, C, PACK], BF16, "woven_first")
-        picked_middle = tile([P, PACK, C], BF16, "picked_middle")
+        woven0 = tile([P, C, PACK], BF16, "woven0")
+        picked1 = tile([P, PACK, C], BF16, "picked1")
         picked_last = tile([P, PACK, 2 * C], BF16, "picked_last")
-        for j in range(PACK):
-            nc.vector.tensor_copy(woven[FIRST][:, :, j], tokens(j, *FIRST))
-            share = (C, C, 0, C // 2)[j]
-            if share:
-                nc.vector.tensor_copy(picked_middle[:, j, 0:share], tokens(j, C, C + share))
-            if share < C:
-                nc.scalar.activation(picked_middle[:, j, share:C], tokens(j, C + share, 2 * C), COPY)
-            nc.scalar.activation(picked_last[:, j, :], tokens(j, *LAST), COPY)
-        quantize(FIRST)
-        products(FIRST)
-        woven[MIDDLE] = tile([P, C, PACK], BF16, "woven_middle")
-        weave(nc.vector.tensor_copy, woven[MIDDLE][:], picked_middle[:])
+        for j in range(PACK - 1):
+            nc.vector.tensor_copy(woven0[:, :, j], tokens(j, 0, C))
+            if j < 2:
+                nc.vector.tensor_copy(picked1[:, j, :], tokens(j, C, 2 * C))
+            else:
+                nc.scalar.activation(picked1[:, j, :], tokens(j, C, 2 * C), COPY)
+            nc.scalar.activation(picked_last[:, j, :], tokens(j, 2 * C, T), COPY)
+        nc.scalar.activation(picked_last[:, 3, :], tokens(3, 2 * C, T), COPY)
+        for h in range(2):
+            nc.vector.tensor_copy(woven0[:, HALF * h : HALF * (h + 1), 3], tokens(3, HALF * h, HALF * (h + 1)))
+        halves = []
+        for h in range(2):
+            lo, hi = HALF * h, HALF * (h + 1)
+            quantize(0, woven0, lo, hi)
+            halves.append(product(0, 0, lo, hi, banks[0][h][:, 0, :]))
+            nc.vector.tensor_copy(picked1[:, 3, lo:hi], tokens(3, C + lo, C + hi))
+
+        def prepare(e, picked):
+            woven = tile([P, C, PACK], BF16, f"woven{e}", "woven_rest")
+            weave(woven[:], picked)
+            codes[e] = tile([P, C], U32, f"codes{e}")
+            quantize(e, woven)
+            return [product(i, e) for i in range(N_TILES)]
+
+        for h in range(2):
+            gated(halves[h], 0, 0, HALF * h, HALF * (h + 1))
+            scalar_scatter(0, HALF * h, HALF * (h + 1))
+        for i in range(1, N_TILES):
+            gated(product(i, 0), i, 0)
+        for i in range(1, 3):
+            scalar_scatter(i, 0, C)
+        accs = prepare(1, picked1[:])
+        vector_scatter(3, 0, C)
         for i in range(N_TILES):
-            gated(i, *FIRST)
-        for i in range(3):
-            scalar_scatter(i, *FIRST)
-        quantize(MIDDLE)
-        products(MIDDLE)
-        woven[LAST] = laid.tile([P, 2 * C, PACK], BF16, name="woven_last", offset=0, align_bytes=64)
-        weave(nc.vector.tensor_copy, woven[LAST][:], picked_last[:])
-        gated(0, *MIDDLE)
-        quantize(LAST)
-        products(LAST)
-        for i in (3, 2):
-            biased(i, *MIDDLE)
-        scalar_scatter(0, *MIDDLE)
-        gated(1, *MIDDLE)
-        gated(0, *LAST)
-        for i in (3, 2):
-            biased(i, *LAST)
-        nc.vector.tensor_copy(windows[3][:].indirect(entries(dst_t, *FIRST)), sums[3][:, FIRST[0] : FIRST[1]])
-        gated(1, *LAST)
-        for scalar_window, vector_window in ((0, 3), (1, 2)):
-            if scalar_window:
-                scalar_scatter(scalar_window, *MIDDLE)
-            vector_scatter(vector_window, *MIDDLE)
-            scalar_scatter(scalar_window, 512, 768)
-            scalar_scatter(scalar_window, 768, 1024)
-            vector_scatter(vector_window, *LAST)
-            store(scalar_window)
-            store(vector_window)
+            gated(accs[i], i, 1)
+        scalar_scatter(0, C, 2 * C)
+        scalar_scatter(2, C, C + HALF)
+        accs = prepare(2, picked_last[:, :, 0:C])
+        vector_scatter(3, C, 2 * C)
+        for i in range(N_TILES):
+            gated(accs[i], i, 2)
+        accs = prepare(3, picked_last[:, :, C : 2 * C])
+        vector_scatter(3, 2 * C, 3 * C)
+        for i in range(N_TILES):
+            gated(accs[i], i, 3)
+        vector_scatter(3, 3 * C, T)
+        store(3)
+        scalar_scatter(0, 2 * C, 3 * C)
+        scalar_scatter(0, 3 * C, T)
+        scalar_scatter(1, C, C + 384)
+        store(0)
+        scalar_scatter(1, C + 384, T)
+        store(1)
+        vector_scatter(2, C + HALF, T)
+        store(2)

@@ -24,6 +24,7 @@ MULT = mybir.AluOpType.mult
 ADD = mybir.AluOpType.add
 
 HALF = C // 2
+SHARE = 576
 
 
 def tile_moe_two_lin_bias_kernel(tc, xT, w_words, w_scales, b, gate, offs, dst, out):
@@ -42,25 +43,28 @@ def tile_moe_two_lin_bias_kernel(tc, xT, w_words, w_scales, b, gate, offs, dst, 
         word_rows = w_words.rearrange("e a p n -> p (e a) n").bitcast(I32)
         words = [tile([P, 2 * N], U8, "words0"), tile([P, E - 1, 2 * N], U8, "words_rest")]
         scale_rows = w_scales.rearrange("e a (q r) n -> r (a q) e n", r=4).bitcast(I32)
-        w_scale = tile([P, E, N], U8, "w_scale")
+        w_scale = [tile([P, 1, N], U8, "w_scale0"), tile([P, E - 1, N], U8, "w_scale_rest")]
         bias = tile([P, N_TILES, E], F32, "bias")
         gates = [tile([P, C], F32, "gate0", "codes1"), tile([P, T - C], F32, "gate_rest")]
 
         warm = tile([P, 16], F32, "warm")
         nc.gpsimd.memset(warm[:, 0:1], 0.0)
         nc.scalar.activation(warm[:, 8:9], warm[:, 0:1], COPY)
-        nc.vector.memset(w_scale[:].bitcast(I32), 0)
+        for plane in w_scale:
+            nc.vector.memset(plane[:].bitcast(I32), 0)
         nc.sync.dma_start(out=planes[0][:], in_=x_rows[:, 0, :])
         nc.sync.dma_start(offs_t[:], offs)
         nc.sync.dma_start(dst_t[:], dst)
         for j in range(1, PACK):
             nc.sync.dma_start(out=planes[j][:], in_=x_rows[:, j, :])
         nc.sync.dma_start(out=words[0][:].bitcast(I32), in_=word_rows[:, 0])
-        nc.sync.dma_start(out=bias[:], in_=b.rearrange("(i p) e -> p i e", p=P))
-        for r in range(4):
-            nc.sync.dma_start(out=w_scale[r:P:32].bitcast(I32), in_=scale_rows[r])
         nc.sync.dma_start(out=gates[0][:], in_=gate[0:P, 0:C])
+        for r in range(4):
+            nc.sync.dma_start(out=w_scale[0][r:P:32].bitcast(I32), in_=scale_rows[r][:, 0:1])
+        nc.sync.dma_start(out=bias[:], in_=b.rearrange("(i p) e -> p i e", p=P))
         nc.sync.dma_start(out=words[1][:].bitcast(I32), in_=word_rows[:, 1:E])
+        for r in range(4):
+            nc.sync.dma_start(out=w_scale[1][r:P:32].bitcast(I32), in_=scale_rows[r][:, 1:E])
         nc.sync.dma_start(out=gates[1][:], in_=gate[0:P, C:T])
 
         windows = [tile([P, T], F32, f"window{i}") for i in range(N_TILES)]
@@ -92,7 +96,7 @@ def tile_moe_two_lin_bias_kernel(tc, xT, w_words, w_scales, b, gate, offs, dst, 
             nc.tensor.matmul_mx(
                 out=acc[:, lo:hi],
                 lhsT=(words[1][:, e - 1, columns] if e else words[0][:, columns]).bitcast(FP4X4),
-                lhsT_scale=w_scale[:, e, P * i : P * (i + 1)],
+                lhsT_scale=w_scale[min(e, 1)][:, max(e - 1, 0), P * i : P * (i + 1)],
                 rhs=codes[e][:, lo:hi].bitcast(FP8X4),
                 rhs_scale=scales[e][:, lo:hi],
                 start=True,
@@ -114,7 +118,7 @@ def tile_moe_two_lin_bias_kernel(tc, xT, w_words, w_scales, b, gate, offs, dst, 
             nc.vector.tensor_copy(windows[i][:].indirect(entries(dst_t, lo, hi)), sums[i][:, lo:hi])
 
         def store(i):
-            (nc.scalar if i < 2 else nc.sync).dma_start(out=out[P * i : P * (i + 1), :], in_=windows[i][:])
+            (nc.scalar if i == 1 else nc.sync).dma_start(out=out[P * i : P * (i + 1), :], in_=windows[i][:])
 
         woven0 = tile([P, C, PACK], BF16, "woven0")
         picked1 = tile([P, PACK, C], BF16, "picked1")
@@ -136,41 +140,42 @@ def tile_moe_two_lin_bias_kernel(tc, xT, w_words, w_scales, b, gate, offs, dst, 
             halves.append(product(0, 0, lo, hi, banks[0][h][:, 0, :]))
             nc.vector.tensor_copy(picked1[:, 3, lo:hi], tokens(3, C + lo, C + hi))
 
-        def prepare(e, picked):
+        def prepare(e, picked, order=range(N_TILES)):
             woven = tile([P, C, PACK], BF16, f"woven{e}", "woven_rest")
             weave(woven[:], picked)
             codes[e] = tile([P, C], U32, f"codes{e}")
             quantize(e, woven)
-            return [product(i, e) for i in range(N_TILES)]
+            return {i: product(i, e) for i in order}
 
         for h in range(2):
             gated(halves[h], 0, 0, HALF * h, HALF * (h + 1))
             scalar_scatter(0, HALF * h, HALF * (h + 1))
         for i in range(1, N_TILES):
             gated(product(i, 0), i, 0)
-        for i in range(1, 3):
-            scalar_scatter(i, 0, C)
+        scalar_scatter(1, 0, C)
+        scalar_scatter(2, 0, C)
         accs = prepare(1, picked1[:])
         vector_scatter(3, 0, C)
         for i in range(N_TILES):
             gated(accs[i], i, 1)
         scalar_scatter(0, C, 2 * C)
-        scalar_scatter(2, C, C + HALF)
+        scalar_scatter(1, C, 2 * C)
         accs = prepare(2, picked_last[:, :, 0:C])
         vector_scatter(3, C, 2 * C)
         for i in range(N_TILES):
             gated(accs[i], i, 2)
-        accs = prepare(3, picked_last[:, :, C : 2 * C])
+        scalar_scatter(0, 2 * C, 3 * C)
+        scalar_scatter(2, C, SHARE)
+        accs = prepare(3, picked_last[:, :, C : 2 * C], (1, 3, 0, 2))
         vector_scatter(3, 2 * C, 3 * C)
-        for i in range(N_TILES):
+        for i in accs:
             gated(accs[i], i, 3)
         vector_scatter(3, 3 * C, T)
         store(3)
-        scalar_scatter(0, 2 * C, 3 * C)
-        scalar_scatter(0, 3 * C, T)
-        scalar_scatter(1, C, C + 384)
+        vector_scatter(0, 3 * C, T)
         store(0)
-        scalar_scatter(1, C + 384, T)
+        scalar_scatter(1, 2 * C, T - HALF)
+        scalar_scatter(1, T - HALF, T)
         store(1)
-        vector_scatter(2, C + HALF, T)
+        vector_scatter(2, SHARE, T)
         store(2)

@@ -120,8 +120,9 @@ def tile_moe_two_lin_bias_kernel(tc, xT, w_words, w_scales, b, gate, offs, dst, 
         def store(i):
             (nc.scalar if i == 1 else nc.sync).dma_start(out=out[P * i : P * (i + 1), :], in_=windows[i][:])
 
-        woven0 = tile([P, C, PACK], BF16, "woven0")
-        picked1 = tile([P, PACK, C], BF16, "picked1")
+        stage = tile([P, (2 * PACK - 1) * C], BF16, "stage")
+        picked1 = stage[:, 0 : PACK * C].rearrange("p (j w) -> p j w", j=PACK)
+        woven0 = stage[:, (PACK - 1) * C :].rearrange("p (w j) -> p w j", j=PACK)
         picked_last = tile([P, PACK, 2 * C], BF16, "picked_last")
         for j in range(PACK - 1):
             nc.vector.tensor_copy(woven0[:, :, j], tokens(j, 0, C))
@@ -138,7 +139,7 @@ def tile_moe_two_lin_bias_kernel(tc, xT, w_words, w_scales, b, gate, offs, dst, 
             lo, hi = HALF * h, HALF * (h + 1)
             quantize(0, woven0, lo, hi)
             halves.append(product(0, 0, lo, hi, banks[0][h][:, 0, :]))
-            nc.vector.tensor_copy(picked1[:, 3, lo:hi], tokens(3, C + lo, C + hi))
+        nc.vector.tensor_copy(picked1[:, 3, :], tokens(3, C, 2 * C))
 
         def prepare(e, picked, order=range(N_TILES)):
             woven = tile([P, C, PACK], BF16, f"woven{e}", "woven_rest")
@@ -154,7 +155,7 @@ def tile_moe_two_lin_bias_kernel(tc, xT, w_words, w_scales, b, gate, offs, dst, 
             gated(product(i, 0), i, 0)
         scalar_scatter(1, 0, C)
         scalar_scatter(2, 0, C)
-        accs = prepare(1, picked1[:])
+        accs = prepare(1, picked1)
         vector_scatter(3, 0, C)
         for i in range(N_TILES):
             gated(accs[i], i, 1)

@@ -120,9 +120,8 @@ def tile_moe_two_lin_bias_kernel(tc, xT, w_words, w_scales, b, gate, offs, dst, 
         def store(i):
             (nc.scalar if i == 1 else nc.sync).dma_start(out=out[P * i : P * (i + 1), :], in_=windows[i][:])
 
-        stage = tile([P, (2 * PACK - 1) * C], BF16, "stage")
-        picked1 = stage[:, 0 : PACK * C].rearrange("p (j w) -> p j w", j=PACK)
-        woven0 = stage[:, (PACK - 1) * C :].rearrange("p (w j) -> p w j", j=PACK)
+        woven0 = tile([P, C, PACK], BF16, "woven0")
+        picked1 = tile([P, PACK, C], BF16, "picked1")
         picked_last = tile([P, PACK, 2 * C], BF16, "picked_last")
         for j in range(PACK - 1):
             nc.vector.tensor_copy(woven0[:, :, j], tokens(j, 0, C))
@@ -134,16 +133,19 @@ def tile_moe_two_lin_bias_kernel(tc, xT, w_words, w_scales, b, gate, offs, dst, 
         nc.scalar.activation(picked_last[:, 3, :], tokens(3, 2 * C, T), COPY)
         for h in range(2):
             nc.vector.tensor_copy(woven0[:, HALF * h : HALF * (h + 1), 3], tokens(3, HALF * h, HALF * (h + 1)))
+        nc.vector.tensor_copy(picked1[:, 3, :], tokens(3, C, 2 * C))
         halves = []
         for h in range(2):
             lo, hi = HALF * h, HALF * (h + 1)
             quantize(0, woven0, lo, hi)
             halves.append(product(0, 0, lo, hi, banks[0][h][:, 0, :]))
-        nc.vector.tensor_copy(picked1[:, 3, :], tokens(3, C, 2 * C))
+        woven1 = tile([P, C, PACK], BF16, "woven1", "woven_rest")
+        nc.vector.tensor_copy(woven1[:].rearrange("p (s u) j -> p s j u", u=4), picked1[:].rearrange("p j (s u) -> p s j u", u=4))
 
-        def prepare(e, picked, order=range(N_TILES)):
-            woven = tile([P, C, PACK], BF16, f"woven{e}", "woven_rest")
-            weave(woven[:], picked)
+        def prepare(e, picked, order=range(N_TILES), woven=None):
+            if woven is None:
+                woven = tile([P, C, PACK], BF16, f"woven{e}", "woven_rest")
+                weave(woven[:], picked)
             codes[e] = tile([P, C], U32, f"codes{e}")
             quantize(e, woven)
             return {i: product(i, e) for i in order}
@@ -155,7 +157,7 @@ def tile_moe_two_lin_bias_kernel(tc, xT, w_words, w_scales, b, gate, offs, dst, 
             gated(product(i, 0), i, 0)
         scalar_scatter(1, 0, C)
         scalar_scatter(2, 0, C)
-        accs = prepare(1, picked1)
+        accs = prepare(1, None, woven=woven1)
         vector_scatter(3, 0, C)
         for i in range(N_TILES):
             gated(accs[i], i, 1)

@@ -6,7 +6,6 @@ K, T, E, C, N = 512, 1024, 4, 256, 512
 P = 128
 PACK = 4
 N_TILES = N // P
-BANK = 512
 
 FLOPS = 2 * K * N * E * C
 BYTES = 4 * (K * T + N * E + E * C + N * T) + E * (K * N // 2 + K // 32 * N) + 2 * 2 * P * (T // 16)
@@ -24,7 +23,8 @@ MULT = mybir.AluOpType.mult
 ADD = mybir.AluOpType.add
 
 HALF = C // 2
-SHARE = 576
+SCALAR_SHARE = 576
+SCALAR_WINDOW = 1
 
 
 def tile_moe_two_lin_bias_kernel(tc, xT, w_words, w_scales, b, gate, offs, dst, out):
@@ -33,8 +33,8 @@ def tile_moe_two_lin_bias_kernel(tc, xT, w_words, w_scales, b, gate, offs, dst, 
         held = ctx.enter_context(tc.tile_pool(name="held", bufs=1))
         psum = ctx.enter_context(tc.psum_pool(name="psum", bufs=1))
 
-        def tile(shape, dtype, name, slot=None):
-            return held.tile(shape, dtype, name=name, tag=slot or name, align_bytes=64)
+        def tile(shape, dtype, name, shares=None):
+            return held.tile(shape, dtype, name=name, tag=shares or name, align_bytes=64)
 
         offs_t = held.tile([P, T // 16], U16, name="offs_t")
         dst_t = held.tile([P, T // 16], U16, name="dst_t")
@@ -47,11 +47,12 @@ def tile_moe_two_lin_bias_kernel(tc, xT, w_words, w_scales, b, gate, offs, dst, 
         bias = tile([P, N_TILES, E], F32, "bias")
         gates = [tile([P, C], F32, "gate0", "codes1"), tile([P, T - C], F32, "gate_rest")]
 
-        warm = tile([P, 16], F32, "warm")
-        nc.gpsimd.memset(warm[:, 0:1], 0.0)
-        nc.scalar.activation(warm[:, 8:9], warm[:, 0:1], COPY)
-        for plane in w_scale:
-            nc.vector.memset(plane[:].bitcast(I32), 0)
+        for scale_tile in w_scale:
+            nc.vector.memset(scale_tile[:].bitcast(I32), 0)
+
+        warm = tile([P, 1], F32, "warm")
+        nc.scalar.activation(warm[:], w_scale[1][:, 0, 0:4].bitcast(F32), COPY)
+
         nc.sync.dma_start(out=planes[0][:], in_=x_rows[:, 0, :])
         nc.sync.dma_start(offs_t[:], offs)
         nc.sync.dma_start(dst_t[:], dst)
@@ -71,6 +72,7 @@ def tile_moe_two_lin_bias_kernel(tc, xT, w_words, w_scales, b, gate, offs, dst, 
         sums = [tile([P, T], F32, f"sums{i}") for i in range(N_TILES)]
         codes = {0: tile([P, C], U32, "codes0")}
         scales = [tile([P, C], U8, f"scales{e}") for e in range(E)]
+        banks = [[psum.tile([P, 2, C], F32, name=f"bank{i}_{h}") for h in range(2)] for i in range(N_TILES)]
 
         def entries(listed, lo, hi):
             return listed[:, lo // 16 : hi // 16]
@@ -78,17 +80,12 @@ def tile_moe_two_lin_bias_kernel(tc, xT, w_words, w_scales, b, gate, offs, dst, 
         def tokens(j, lo, hi):
             return planes[j][:].indirect(entries(offs_t, lo, hi))
 
-        def weave(into, picked):
-            nc.gpsimd.tensor_scalar(into, picked.rearrange("p j w -> p w j"), 1.0, 0.0, op0=MULT, op1=ADD)
-
         def quantize(e, woven, lo=0, hi=C):
             nc.vector.quantize_mx(
                 out=codes[e][:, lo:hi].bitcast(FP8X4),
                 scales=scales[e][:, lo:hi],
                 in_=woven[:, lo:hi, :].rearrange("p w j -> p (w j)"),
             )
-
-        banks = [[psum.tile([P, 2, C], F32, name=f"bank{i}_{h}") for h in range(2)] for i in range(N_TILES)]
 
         def product(i, e, lo=0, hi=C, acc=None):
             acc = banks[i][e // 2][:, e % 2, :] if acc is None else acc
@@ -104,12 +101,20 @@ def tile_moe_two_lin_bias_kernel(tc, xT, w_words, w_scales, b, gate, offs, dst, 
             )
             return acc
 
-        def gate_of(e):
-            return gates[1][:, C * (e - 1) : C * e] if e else gates[0]
+        def multiply(e, woven, order=range(N_TILES)):
+            codes[e] = tile([P, C], U32, f"codes{e}")
+            quantize(e, woven)
+            return {i: product(i, e) for i in order}
+
+        def weave_on_gpsimd(e, picked):
+            woven = tile([P, C, PACK], BF16, f"woven{e}", "woven_rest")
+            nc.gpsimd.tensor_scalar(woven[:], picked.rearrange("p j w -> p w j"), 1.0, 0.0, op0=MULT, op1=ADD)
+            return woven
 
         def gated(acc, i, e, lo=0, hi=C):
+            weight = gates[1][:, C * (e - 1) : C * e] if e else gates[0]
             slots = slice(C * e + lo, C * e + hi)
-            nc.vector.scalar_tensor_tensor(sums[i][:, slots], acc[:, lo:hi], bias[:, i, e : e + 1], gate_of(e)[:, lo:hi], ADD, MULT)
+            nc.vector.scalar_tensor_tensor(sums[i][:, slots], acc[:, lo:hi], bias[:, i, e : e + 1], weight[:, lo:hi], ADD, MULT)
 
         def scalar_scatter(i, lo, hi):
             nc.scalar.activation(windows[i][:].indirect(entries(dst_t, lo, hi)), sums[i][:, lo:hi], COPY)
@@ -118,58 +123,57 @@ def tile_moe_two_lin_bias_kernel(tc, xT, w_words, w_scales, b, gate, offs, dst, 
             nc.vector.tensor_copy(windows[i][:].indirect(entries(dst_t, lo, hi)), sums[i][:, lo:hi])
 
         def store(i):
-            (nc.scalar if i == 1 else nc.sync).dma_start(out=out[P * i : P * (i + 1), :], in_=windows[i][:])
+            queue = nc.scalar if i == SCALAR_WINDOW else nc.sync
+            queue.dma_start(out=out[P * i : P * (i + 1), :], in_=windows[i][:])
 
         woven0 = tile([P, C, PACK], BF16, "woven0")
         picked1 = tile([P, PACK, C], BF16, "picked1")
         picked_last = tile([P, PACK, 2 * C], BF16, "picked_last")
-        for j in range(PACK - 1):
+        last = PACK - 1
+        for j in range(last):
             nc.vector.tensor_copy(woven0[:, :, j], tokens(j, 0, C))
-            if j < 2:
+            if j < last - 1:
                 nc.vector.tensor_copy(picked1[:, j, :], tokens(j, C, 2 * C))
             else:
                 nc.scalar.activation(picked1[:, j, :], tokens(j, C, 2 * C), COPY)
             nc.scalar.activation(picked_last[:, j, :], tokens(j, 2 * C, T), COPY)
-        nc.scalar.activation(picked_last[:, 3, :], tokens(3, 2 * C, T), COPY)
-        for h in range(2):
-            nc.vector.tensor_copy(woven0[:, HALF * h : HALF * (h + 1), 3], tokens(3, HALF * h, HALF * (h + 1)))
-        nc.vector.tensor_copy(picked1[:, 3, :], tokens(3, C, 2 * C))
-        halves = []
-        for h in range(2):
-            lo, hi = HALF * h, HALF * (h + 1)
+        nc.scalar.activation(picked_last[:, last, :], tokens(last, 2 * C, T), COPY)
+
+        halves = [(HALF * h, HALF * (h + 1)) for h in range(2)]
+        for lo, hi in halves:
+            nc.vector.tensor_copy(woven0[:, lo:hi, last], tokens(last, lo, hi))
+        nc.vector.tensor_copy(picked1[:, last, :], tokens(last, C, 2 * C))
+        opening = []
+        for h, (lo, hi) in enumerate(halves):
             quantize(0, woven0, lo, hi)
-            halves.append(product(0, 0, lo, hi, banks[0][h][:, 0, :]))
+            opening.append(product(0, 0, lo, hi, banks[0][h][:, 0, :]))
+
         woven1 = tile([P, C, PACK], BF16, "woven1", "woven_rest")
         nc.vector.tensor_copy(woven1[:].rearrange("p (s u) j -> p s j u", u=4), picked1[:].rearrange("p j (s u) -> p s j u", u=4))
 
-        def prepare(e, picked, order=range(N_TILES), woven=None):
-            if woven is None:
-                woven = tile([P, C, PACK], BF16, f"woven{e}", "woven_rest")
-                weave(woven[:], picked)
-            codes[e] = tile([P, C], U32, f"codes{e}")
-            quantize(e, woven)
-            return {i: product(i, e) for i in order}
-
-        for h in range(2):
-            gated(halves[h], 0, 0, HALF * h, HALF * (h + 1))
-            scalar_scatter(0, HALF * h, HALF * (h + 1))
+        for acc, (lo, hi) in zip(opening, halves):
+            gated(acc, 0, 0, lo, hi)
+            scalar_scatter(0, lo, hi)
         for i in range(1, N_TILES):
             gated(product(i, 0), i, 0)
         scalar_scatter(1, 0, C)
         scalar_scatter(2, 0, C)
-        accs = prepare(1, None, woven=woven1)
+
+        accs = multiply(1, woven1)
         vector_scatter(3, 0, C)
-        for i in range(N_TILES):
+        for i in accs:
             gated(accs[i], i, 1)
         scalar_scatter(0, C, 2 * C)
         scalar_scatter(1, C, 2 * C)
-        accs = prepare(2, picked_last[:, :, 0:C])
+
+        accs = multiply(2, weave_on_gpsimd(2, picked_last[:, :, 0:C]))
         vector_scatter(3, C, 2 * C)
-        for i in range(N_TILES):
+        for i in accs:
             gated(accs[i], i, 2)
         scalar_scatter(0, 2 * C, 3 * C)
-        scalar_scatter(2, C, SHARE)
-        accs = prepare(3, picked_last[:, :, C : 2 * C], (1, 3, 0, 2))
+        scalar_scatter(2, C, SCALAR_SHARE)
+
+        accs = multiply(3, weave_on_gpsimd(3, picked_last[:, :, C : 2 * C]), (SCALAR_WINDOW, 3, 0, 2))
         vector_scatter(3, 2 * C, 3 * C)
         for i in accs:
             gated(accs[i], i, 3)
@@ -177,8 +181,8 @@ def tile_moe_two_lin_bias_kernel(tc, xT, w_words, w_scales, b, gate, offs, dst, 
         store(3)
         vector_scatter(0, 3 * C, T)
         store(0)
-        scalar_scatter(1, 2 * C, T - HALF)
-        scalar_scatter(1, T - HALF, T)
-        store(1)
-        vector_scatter(2, SHARE, T)
+        scalar_scatter(SCALAR_WINDOW, 2 * C, T - HALF)
+        scalar_scatter(SCALAR_WINDOW, T - HALF, T)
+        store(SCALAR_WINDOW)
+        vector_scatter(2, SCALAR_SHARE, T)
         store(2)

@@ -23,7 +23,7 @@ MULT = mybir.AluOpType.mult
 ADD = mybir.AluOpType.add
 
 HALF = C // 2
-SCALAR_SHARE = 576
+SCALAR_SHARE = 544
 SCALAR_WINDOW = 1
 
 
@@ -151,13 +151,15 @@ def tile_moe_two_lin_bias_kernel(tc, xT, w_words, w_scales, b, gate, offs, dst, 
         woven1 = tile([P, C, PACK], BF16, "woven1", "woven_rest")
         nc.vector.tensor_copy(woven1[:].rearrange("p (s u) j -> p s j u", u=4), picked1[:].rearrange("p j (s u) -> p s j u", u=4))
 
-        for acc, (lo, hi) in zip(opening, halves):
-            gated(acc, 0, 0, lo, hi)
-            scalar_scatter(0, lo, hi)
-        for i in range(1, N_TILES):
-            gated(product(i, 0), i, 0)
+        gated(opening[0], 0, 0, *halves[0])
+        scalar_scatter(0, *halves[0])
+        gated(product(1, 0), 1, 0)
         scalar_scatter(1, 0, C)
+        gated(opening[1], 0, 0, *halves[1])
+        scalar_scatter(0, *halves[1])
+        gated(product(2, 0), 2, 0)
         scalar_scatter(2, 0, C)
+        gated(product(3, 0), 3, 0)
 
         accs = multiply(1, woven1)
         vector_scatter(3, 0, C)
@@ -171,6 +173,7 @@ def tile_moe_two_lin_bias_kernel(tc, xT, w_words, w_scales, b, gate, offs, dst, 
         for i in accs:
             gated(accs[i], i, 2)
         scalar_scatter(0, 2 * C, 3 * C)
+        scalar_scatter(SCALAR_WINDOW, 2 * C, 2 * C + HALF)
         scalar_scatter(2, C, SCALAR_SHARE)
 
         accs = multiply(3, weave_on_gpsimd(3, picked_last[:, :, C : 2 * C]), (SCALAR_WINDOW, 3, 0, 2))
@@ -181,8 +184,7 @@ def tile_moe_two_lin_bias_kernel(tc, xT, w_words, w_scales, b, gate, offs, dst, 
         store(3)
         vector_scatter(0, 3 * C, T)
         store(0)
-        scalar_scatter(SCALAR_WINDOW, 2 * C, T - HALF)
-        scalar_scatter(SCALAR_WINDOW, T - HALF, T)
+        scalar_scatter(SCALAR_WINDOW, 2 * C + HALF, T)
         store(SCALAR_WINDOW)
         vector_scatter(2, SCALAR_SHARE, T)
         store(2)

@@ -23,7 +23,7 @@ MULT = mybir.AluOpType.mult
 ADD = mybir.AluOpType.add
 
 HALF = C // 2
-SCALAR_SHARE = 544
+SCALAR_SHARE = 640
 SCALAR_WINDOW = 1
 
 

@@ -23,7 +23,7 @@ MULT = mybir.AluOpType.mult
 ADD = mybir.AluOpType.add
 
 HALF = C // 2
-SCALAR_SHARE = 640
+SCALAR_SHARE = 608
 SCALAR_WINDOW = 1
 
 
@@ -44,8 +44,8 @@ def tile_moe_two_lin_bias_kernel(tc, xT, w_words, w_scales, b, gate, offs, dst, 
         words = [tile([P, 2 * N], U8, "words0"), tile([P, E - 1, 2 * N], U8, "words_rest")]
         scale_rows = w_scales.rearrange("e a (q r) n -> r (a q) e n", r=4).bitcast(I32)
         w_scale = [tile([P, 1, N], U8, "w_scale0"), tile([P, E - 1, N], U8, "w_scale_rest")]
-        bias = tile([P, N_TILES, E], F32, "bias")
-        gates = [tile([P, C], F32, "gate0", "codes1"), tile([P, T - C], F32, "gate_rest")]
+        bias = tile([P, N_TILES, 2 * E], F32, "bias")
+        gates = [tile([P, C], F32, "gate0", "gate0"), tile([P, C], F32, "gate1"), tile([P, 2 * C], F32, "gate_rest")]
 
         for scale_tile in w_scale:
             nc.vector.memset(scale_tile[:].bitcast(I32), 0)
@@ -62,16 +62,17 @@ def tile_moe_two_lin_bias_kernel(tc, xT, w_words, w_scales, b, gate, offs, dst, 
         nc.sync.dma_start(out=gates[0][:], in_=gate[0:P, 0:C])
         for r in range(4):
             nc.sync.dma_start(out=w_scale[0][r:P:32].bitcast(I32), in_=scale_rows[r][:, 0:1])
-        nc.sync.dma_start(out=bias[:], in_=b.rearrange("(i p) e -> p i e", p=P))
+        nc.sync.dma_start(out=bias[:, :, 0:E], in_=b.rearrange("(i p) e -> p i e", p=P))
+        nc.sync.dma_start(out=gates[1][:], in_=gate[0:P, C : 2 * C])
         nc.sync.dma_start(out=words[1][:].bitcast(I32), in_=word_rows[:, 1:E])
         for r in range(4):
             nc.sync.dma_start(out=w_scale[1][r:P:32].bitcast(I32), in_=scale_rows[r][:, 1:E])
-        nc.sync.dma_start(out=gates[1][:], in_=gate[0:P, C:T])
+        nc.sync.dma_start(out=gates[2][:], in_=gate[0:P, 2 * C : T])
 
         windows = [tile([P, T], F32, f"window{i}") for i in range(N_TILES)]
         sums = [tile([P, T], F32, f"sums{i}") for i in range(N_TILES)]
-        codes = {0: tile([P, C], U32, "codes0")}
-        scales = [tile([P, C], U8, f"scales{e}") for e in range(E)]
+        codes = {0: tile([P, C], U32, "codes0", "codes")}
+        scales = [tile([P, C], U8, f"scales{e}", "gate0" if e == 1 else None) for e in range(E)]
         banks = [[psum.tile([P, 2, C], F32, name=f"bank{i}_{h}") for h in range(2)] for i in range(N_TILES)]
 
         def entries(listed, lo, hi):
@@ -84,7 +85,7 @@ def tile_moe_two_lin_bias_kernel(tc, xT, w_words, w_scales, b, gate, offs, dst, 
             nc.vector.quantize_mx(
                 out=codes[e][:, lo:hi].bitcast(FP8X4),
                 scales=scales[e][:, lo:hi],
-                in_=woven[:, lo:hi, :].rearrange("p w j -> p (w j)"),
+                in_=woven.rearrange("p w j -> p (w j)"),
             )
 
         def product(i, e, lo=0, hi=C, acc=None):
@@ -102,17 +103,21 @@ def tile_moe_two_lin_bias_kernel(tc, xT, w_words, w_scales, b, gate, offs, dst, 
             return acc
 
         def multiply(e, woven, order=range(N_TILES)):
-            codes[e] = tile([P, C], U32, f"codes{e}")
-            quantize(e, woven)
+            codes[e] = tile([P, C], U32, f"codes{e}", "codes")
+            quantize(e, woven[:])
             return {i: product(i, e) for i in order}
 
-        def weave_on_gpsimd(e, picked):
+        def weave_on_gpsimd(e, parts):
             woven = tile([P, C, PACK], BF16, f"woven{e}", "woven_rest")
-            nc.gpsimd.tensor_scalar(woven[:], picked.rearrange("p j w -> p w j"), 1.0, 0.0, op0=MULT, op1=ADD)
+            for planes_of, source in parts:
+                nc.gpsimd.tensor_scalar(woven[:, :, planes_of], source, 1.0, 0.0, op0=MULT, op1=ADD)
             return woven
 
+        def picked_of(e, count=PACK):
+            return slice(0, count), picked[:, 0:count, C * (e - 1) : C * e].rearrange("p j w -> p w j")
+
         def gated(acc, i, e, lo=0, hi=C):
-            weight = gates[1][:, C * (e - 1) : C * e] if e else gates[0]
+            weight = gates[2][:, C * (e - 2) : C * (e - 1)] if e > 1 else gates[e]
             slots = slice(C * e + lo, C * e + hi)
             nc.vector.scalar_tensor_tensor(sums[i][:, slots], acc[:, lo:hi], bias[:, i, e : e + 1], weight[:, lo:hi], ADD, MULT)
 
@@ -126,30 +131,29 @@ def tile_moe_two_lin_bias_kernel(tc, xT, w_words, w_scales, b, gate, offs, dst, 
             queue = nc.scalar if i == SCALAR_WINDOW else nc.sync
             queue.dma_start(out=out[P * i : P * (i + 1), :], in_=windows[i][:])
 
+        halves = [(HALF * h, HALF * (h + 1)) for h in range(2)]
         woven0 = tile([P, C, PACK], BF16, "woven0")
-        picked1 = tile([P, PACK, C], BF16, "picked1")
-        picked_last = tile([P, PACK, 2 * C], BF16, "picked_last")
+        picked = tile([P, PACK, T - C], BF16, "picked")
         last = PACK - 1
         for j in range(last):
             nc.vector.tensor_copy(woven0[:, :, j], tokens(j, 0, C))
             if j < last - 1:
-                nc.vector.tensor_copy(picked1[:, j, :], tokens(j, C, 2 * C))
+                nc.vector.tensor_copy(picked[:, j, 0:C], tokens(j, C, 2 * C))
             else:
-                nc.scalar.activation(picked1[:, j, :], tokens(j, C, 2 * C), COPY)
-            nc.scalar.activation(picked_last[:, j, :], tokens(j, 2 * C, T), COPY)
-        nc.scalar.activation(picked_last[:, last, :], tokens(last, 2 * C, T), COPY)
+                nc.scalar.activation(picked[:, j, 0:C], tokens(j, C, 2 * C), COPY)
+            nc.scalar.activation(picked[:, j, C:], tokens(j, 2 * C, T), COPY)
+        for e in (1, 2):
+            nc.scalar.activation(picked[:, last, C * (e - 1) : C * e], tokens(last, C * e, C * (e + 1)), COPY)
 
-        halves = [(HALF * h, HALF * (h + 1)) for h in range(2)]
         for lo, hi in halves:
             nc.vector.tensor_copy(woven0[:, lo:hi, last], tokens(last, lo, hi))
-        nc.vector.tensor_copy(picked1[:, last, :], tokens(last, C, 2 * C))
         opening = []
         for h, (lo, hi) in enumerate(halves):
-            quantize(0, woven0, lo, hi)
+            quantize(0, woven0[:, lo:hi, :], lo, hi)
             opening.append(product(0, 0, lo, hi, banks[0][h][:, 0, :]))
 
-        woven1 = tile([P, C, PACK], BF16, "woven1", "woven_rest")
-        nc.vector.tensor_copy(woven1[:].rearrange("p (s u) j -> p s j u", u=4), picked1[:].rearrange("p j (s u) -> p s j u", u=4))
+        picked_late = tile([P, C], BF16, "picked_late", "woven0")
+        nc.vector.tensor_copy(picked_late[:], tokens(last, 3 * C, T))
 
         gated(opening[0], 0, 0, *halves[0])
         scalar_scatter(0, *halves[0])
@@ -157,18 +161,20 @@ def tile_moe_two_lin_bias_kernel(tc, xT, w_words, w_scales, b, gate, offs, dst, 
         scalar_scatter(1, 0, C)
         gated(opening[1], 0, 0, *halves[1])
         scalar_scatter(0, *halves[1])
+        gated(product(3, 0), 3, 0)
         gated(product(2, 0), 2, 0)
         scalar_scatter(2, 0, C)
-        gated(product(3, 0), 3, 0)
 
+        woven1 = weave_on_gpsimd(1, [picked_of(1)])
+        vector_scatter(3, 0, HALF)
         accs = multiply(1, woven1)
-        vector_scatter(3, 0, C)
+        vector_scatter(3, HALF, C)
         for i in accs:
             gated(accs[i], i, 1)
         scalar_scatter(0, C, 2 * C)
         scalar_scatter(1, C, 2 * C)
 
-        accs = multiply(2, weave_on_gpsimd(2, picked_last[:, :, 0:C]))
+        accs = multiply(2, weave_on_gpsimd(2, [picked_of(2)]))
         vector_scatter(3, C, 2 * C)
         for i in accs:
             gated(accs[i], i, 2)
@@ -176,7 +182,7 @@ def tile_moe_two_lin_bias_kernel(tc, xT, w_words, w_scales, b, gate, offs, dst, 
         scalar_scatter(SCALAR_WINDOW, 2 * C, 2 * C + HALF)
         scalar_scatter(2, C, SCALAR_SHARE)
 
-        accs = multiply(3, weave_on_gpsimd(3, picked_last[:, :, C : 2 * C]), (SCALAR_WINDOW, 3, 0, 2))
+        accs = multiply(3, weave_on_gpsimd(3, [picked_of(3, last), (last, picked_late[:])]), (SCALAR_WINDOW, 3, 0, 2))
         vector_scatter(3, 2 * C, 3 * C)
         for i in accs:
             gated(accs[i], i, 3)

from contextlib import ExitStack

import concourse.mybir as mybir

K, T, E, C, N = 512, 1024, 4, 256, 512
P = 128
PACK = 4
N_TILES = N // P

FLOPS = 2 * K * N * E * C
BYTES = 4 * (K * T + N * E + E * C + N * T) + E * (K * N // 2 + K // 32 * N) + 2 * 2 * P * (T // 16)

F32 = mybir.dt.float32
BF16 = mybir.dt.bfloat16
U32 = mybir.dt.uint32
I32 = mybir.dt.int32
U16 = mybir.dt.uint16
U8 = mybir.dt.uint8
FP8X4 = mybir.dt.float8_e4m3fn_x4
FP4X4 = mybir.dt.float4_e2m1fn_x4
COPY = mybir.ActivationFunctionType.Copy
MULT = mybir.AluOpType.mult
ADD = mybir.AluOpType.add

HALF = C // 2
SCALAR_SHARE = 608
SCALAR_WINDOW = 1


def tile_moe_two_lin_bias_kernel(tc, xT, w_words, w_scales, b, gate, offs, dst, out):
    nc = tc.nc
    with ExitStack() as ctx:
        held = ctx.enter_context(tc.tile_pool(name="held", bufs=1))
        psum = ctx.enter_context(tc.psum_pool(name="psum", bufs=1))

        def tile(shape, dtype, name, shares=None):
            return held.tile(shape, dtype, name=name, tag=shares or name, align_bytes=64)

        offs_t = held.tile([P, T // 16], U16, name="offs_t")
        dst_t = held.tile([P, T // 16], U16, name="dst_t")
        x_rows = xT.rearrange("(p j) w -> p j w", j=PACK)
        planes = [tile([P, T], F32, f"plane{j}") for j in range(PACK)]
        word_rows = w_words.rearrange("e a p n -> p (e a) n").bitcast(I32)
        words = [tile([P, 2 * N], U8, "words0"), tile([P, E - 1, 2 * N], U8, "words_rest")]
        scale_rows = w_scales.rearrange("e a (q r) n -> r (a q) e n", r=4).bitcast(I32)
        w_scale = [tile([P, 1, N], U8, "w_scale0"), tile([P, E - 1, N], U8, "w_scale_rest")]
        bias = tile([P, N_TILES, 2 * E], F32, "bias")
        gates = [tile([P, C], F32, "gate0", "gate0"), tile([P, C], F32, "gate1"), tile([P, 2 * C], F32, "gate_rest")]

        for scale_tile in w_scale:
            nc.vector.memset(scale_tile[:].bitcast(I32), 0)

        warm = tile([P, 1], F32, "warm")
        nc.scalar.activation(warm[:], w_scale[1][:, 0, 0:4].bitcast(F32), COPY)

        nc.sync.dma_start(out=planes[0][:], in_=x_rows[:, 0, :])
        nc.sync.dma_start(offs_t[:], offs)
        nc.sync.dma_start(dst_t[:], dst)
        for j in range(1, PACK):
            nc.sync.dma_start(out=planes[j][:], in_=x_rows[:, j, :])
        nc.sync.dma_start(out=words[0][:].bitcast(I32), in_=word_rows[:, 0])
        nc.sync.dma_start(out=gates[0][:], in_=gate[0:P, 0:C])
        for r in range(4):
            nc.sync.dma_start(out=w_scale[0][r:P:32].bitcast(I32), in_=scale_rows[r][:, 0:1])
        nc.sync.dma_start(out=bias[:, :, 0:E], in_=b.rearrange("(i p) e -> p i e", p=P))
        nc.sync.dma_start(out=gates[1][:], in_=gate[0:P, C : 2 * C])
        nc.sync.dma_start(out=words[1][:].bitcast(I32), in_=word_rows[:, 1:E])
        for r in range(4):
            nc.sync.dma_start(out=w_scale[1][r:P:32].bitcast(I32), in_=scale_rows[r][:, 1:E])
        nc.sync.dma_start(out=gates[2][:], in_=gate[0:P, 2 * C : T])

        windows = [tile([P, T], F32, f"window{i}") for i in range(N_TILES)]
        sums = [tile([P, T], F32, f"sums{i}") for i in range(N_TILES)]
        codes = {0: tile([P, C], U32, "codes0", "codes")}
        scales = [tile([P, C], U8, f"scales{e}", "gate0" if e == 1 else None) for e in range(E)]
        banks = [[psum.tile([P, 2, C], F32, name=f"bank{i}_{h}") for h in range(2)] for i in range(N_TILES)]

        def entries(listed, lo, hi):
            return listed[:, lo // 16 : hi // 16]

        def tokens(j, lo, hi):
            return planes[j][:].indirect(entries(offs_t, lo, hi))

        def quantize(e, woven, lo=0, hi=C):
            nc.vector.quantize_mx(
                out=codes[e][:, lo:hi].bitcast(FP8X4),
                scales=scales[e][:, lo:hi],
                in_=woven.rearrange("p w j -> p (w j)"),
            )

        def product(i, e, lo=0, hi=C, acc=None):
            acc = banks[i][e // 2][:, e % 2, :] if acc is None else acc
            columns = slice(2 * P * i, 2 * P * (i + 1))
            nc.tensor.matmul_mx(
                out=acc[:, lo:hi],
                lhsT=(words[1][:, e - 1, columns] if e else words[0][:, columns]).bitcast(FP4X4),
                lhsT_scale=w_scale[min(e, 1)][:, max(e - 1, 0), P * i : P * (i + 1)],
                rhs=codes[e][:, lo:hi].bitcast(FP8X4),
                rhs_scale=scales[e][:, lo:hi],
                start=True,
                stop=True,
            )
            return acc

        def multiply(e, woven, order=range(N_TILES)):
            codes[e] = tile([P, C], U32, f"codes{e}", "codes")
            quantize(e, woven[:])
            return {i: product(i, e) for i in order}

        def weave_on_gpsimd(e, parts):
            woven = tile([P, C, PACK], BF16, f"woven{e}", "woven_rest")
            for planes_of, source in parts:
                nc.gpsimd.tensor_scalar(woven[:, :, planes_of], source, 1.0, 0.0, op0=MULT, op1=ADD)
            return woven

        def picked_of(e, count=PACK):
            return slice(0, count), picked[:, 0:count, C * (e - 1) : C * e].rearrange("p j w -> p w j")

        def gated(acc, i, e, lo=0, hi=C):
            weight = gates[2][:, C * (e - 2) : C * (e - 1)] if e > 1 else gates[e]
            slots = slice(C * e + lo, C * e + hi)
            nc.vector.scalar_tensor_tensor(sums[i][:, slots], acc[:, lo:hi], bias[:, i, e : e + 1], weight[:, lo:hi], ADD, MULT)

        def scalar_scatter(i, lo, hi):
            nc.scalar.activation(windows[i][:].indirect(entries(dst_t, lo, hi)), sums[i][:, lo:hi], COPY)

        def vector_scatter(i, lo, hi):
            nc.vector.tensor_copy(windows[i][:].indirect(entries(dst_t, lo, hi)), sums[i][:, lo:hi])

        def store(i):
            queue = nc.scalar if i == SCALAR_WINDOW else nc.sync
            queue.dma_start(out=out[P * i : P * (i + 1), :], in_=windows[i][:])

        halves = [(HALF * h, HALF * (h + 1)) for h in range(2)]
        woven0 = tile([P, C, PACK], BF16, "woven0")
        picked = tile([P, PACK, T - C], BF16, "picked")
        last = PACK - 1
        for j in range(last):
            nc.vector.tensor_copy(woven0[:, :, j], tokens(j, 0, C))
            if j < last - 1:
                nc.vector.tensor_copy(picked[:, j, 0:C], tokens(j, C, 2 * C))
            else:
                nc.scalar.activation(picked[:, j, 0:C], tokens(j, C, 2 * C), COPY)
            nc.scalar.activation(picked[:, j, C:], tokens(j, 2 * C, T), COPY)
        for e in (1, 2):
            nc.scalar.activation(picked[:, last, C * (e - 1) : C * e], tokens(last, C * e, C * (e + 1)), COPY)

        for lo, hi in halves:
            nc.vector.tensor_copy(woven0[:, lo:hi, last], tokens(last, lo, hi))
        opening = []
        for h, (lo, hi) in enumerate(halves):
            quantize(0, woven0[:, lo:hi, :], lo, hi)
            opening.append(product(0, 0, lo, hi, banks[0][h][:, 0, :]))

        picked_late = tile([P, C], BF16, "picked_late", "woven0")
        nc.vector.tensor_copy(picked_late[:], tokens(last, 3 * C, T))

        gated(opening[0], 0, 0, *halves[0])
        scalar_scatter(0, *halves[0])
        gated(product(1, 0), 1, 0)
        scalar_scatter(1, 0, C)
        gated(opening[1], 0, 0, *halves[1])
        scalar_scatter(0, *halves[1])
        gated(product(3, 0), 3, 0)
        gated(product(2, 0), 2, 0)
        scalar_scatter(2, 0, C)

        woven1 = weave_on_gpsimd(1, [picked_of(1)])
        vector_scatter(3, 0, HALF)
        accs = multiply(1, woven1)
        vector_scatter(3, HALF, C)
        for i in accs:
            gated(accs[i], i, 1)
        scalar_scatter(0, C, 2 * C)
        scalar_scatter(1, C, 2 * C)

        accs = multiply(2, weave_on_gpsimd(2, [picked_of(2)]))
        vector_scatter(3, C, 2 * C)
        for i in accs:
            gated(accs[i], i, 2)
        scalar_scatter(0, 2 * C, 3 * C)
        scalar_scatter(SCALAR_WINDOW, 2 * C, 2 * C + HALF)
        scalar_scatter(2, C, SCALAR_SHARE)

        accs = multiply(3, weave_on_gpsimd(3, [picked_of(3, last), (last, picked_late[:])]), (SCALAR_WINDOW, 3, 0, 2))
        vector_scatter(3, 2 * C, 3 * C)
        for i in accs:
            gated(accs[i], i, 3)
        vector_scatter(3, 3 * C, T)
        store(3)
        vector_scatter(0, 3 * C, T)
        store(0)
        scalar_scatter(SCALAR_WINDOW, 2 * C + HALF, T)
        store(SCALAR_WINDOW)
        vector_scatter(2, SCALAR_SHARE, T)
        store(2)
